import numpy as np
import ml_dtypes


def mxq(x, axis, fmt="e4m3"):
    dtype, down = {"e4m3": (ml_dtypes.float8_e4m3fn, 7), "e5m2": (ml_dtypes.float8_e5m2, 14)}[fmt]
    v = np.moveaxis(np.asarray(x, np.float32).astype(ml_dtypes.bfloat16).astype(np.float64), axis, -1)
    blocks = v.reshape(v.shape[:-1] + (-1, 32))
    amax = np.abs(blocks).max(-1, keepdims=True)
    byte = np.maximum(np.where(amax > 0, np.frexp(amax)[1] - 1 + 127, 0) - down, 1)
    scale = np.exp2(byte - 127.0)
    codes = (blocks / scale).astype(np.float32).astype(dtype).astype(np.float64)
    return np.moveaxis((codes * scale).reshape(v.shape), -1, axis)


WIDE = False


def mx_kscale(k):
    if not WIDE:
        return np.ones(k)
    levels = np.array([10, -10, 5, -5, 0])
    if k % 512:
        return np.exp2(np.random.permutation(np.resize(levels, k // 32))).repeat(32)
    a = np.empty((k // 512, 16))
    for p in range(k // 512):
        a[p, :8] = np.random.permutation(np.resize(levels, 8))
        for g in range(8):
            far = levels[np.abs(levels - a[p, g]) >= 10]
            a[p, g + 8] = far[np.random.randint(len(far))]
    return np.exp2(a.ravel()).repeat(32)


def f64(x):
    return np.asarray(x).astype(np.float64)


def striped(idx):
    return np.tile(idx.reshape(-1, 16).T, (8, 1)).astype(np.uint16)


def unstriped(offs):
    return offs[:16].T.reshape(-1).astype(np.int64)


def relu2(v):
    return np.maximum(v, 0.0) ** 2


K, T, E, C, H, N = 512, 1536, 8, 128, 512, 512


def by_expert(wq, xq):
    return np.concatenate([wq[e].T @ xq[:, e * C:(e + 1) * C] for e in range(E)], axis=1)


def setup_inputs():
    n = np.random.standard_normal
    s = mx_kscale(K)[:, None]
    u = mx_kscale(H)
    return {
        "xT": (n((K, T)) * s).astype(np.float32),
        "w1": (n((E + 1, K, H)) / np.sqrt(K) / s[None] * u[None, None, :]).astype(np.float32),
        "w2": (n((E + 1, H, N)) / np.sqrt(H) / u[None, :, None] ** 2).astype(np.float32),
        "gate": np.tile(np.random.uniform(0.2, 1.0, E * C), (N, 1)).astype(np.float32),
        "offs": striped(np.random.permutation(T)[:E * C]),
    }


def reference(xT, w1, w2, gate, offs):
    idx = unstriped(offs)
    w1q, w2q = mxq(f64(w1), 1, "e4m3"), mxq(f64(w2), 1, "e4m3")
    xs = mxq(f64(xT), 0, "e4m3")
    hs = relu2(w1q[E].T @ xs)
    ys = w2q[E].T @ mxq(hs, 0, "e4m3")
    xq = mxq(f64(xT)[:, idx], 0, "e4m3")
    h = relu2(by_expert(w1q, xq))
    y = by_expert(w2q, mxq(h, 0, "e4m3"))
    out = ys
    out[:, idx] += f64(gate) * y
    return out

@@ -1,0 +1,246 @@
+from contextlib import ExitStack
+
+import concourse.mybir as mybir
+
+K, T, E, C, H, N = 512, 1536, 8, 128, 512, 512
+S = E * C
+FLOPS = 2 * (S + T) * (K * H + H * N)
+BYTES = 4 * (K * T + (E + 1) * (K * H + H * N) + S + N * T) + 2 * 128 * (S // 16)
+
+F32 = mybir.dt.float32
+BF16 = mybir.dt.bfloat16
+U32 = mybir.dt.uint32
+U16 = mybir.dt.uint16
+U8 = mybir.dt.uint8
+FP8X4 = mybir.dt.float8_e4m3fn_x4
+ADD, MULT = mybir.AluOpType.add, mybir.AluOpType.mult
+RELU = mybir.ActivationFunctionType.Relu
+SQUARE = mybir.ActivationFunctionType.Square
+
+P = 128
+PACK = 4
+HALF = 512
+PIECE = 256
+CHUNK = 512
+
+
+def tile_moe_shr_mlp_relu2_kernel(tc, xT, w1, w2, gate, offs, out):
+    nc = tc.nc
+    with ExitStack() as ctx:
+        held = ctx.enter_context(tc.tile_pool(name="held", bufs=1))
+        rawp = ctx.enter_context(tc.tile_pool(name="rawp", bufs=7))
+        wbp = ctx.enter_context(tc.tile_pool(name="wbp", bufs=4))
+        wcp = ctx.enter_context(tc.tile_pool(name="wcp", bufs=6))
+        two = ctx.enter_context(tc.tile_pool(name="two", bufs=2))
+        three = ctx.enter_context(tc.tile_pool(name="three", bufs=3))
+        outp = ctx.enter_context(tc.tile_pool(name="outp", bufs=4))
+        ps_a = ctx.enter_context(tc.psum_pool(name="ps_a", bufs=2))
+        ps_y = ctx.enter_context(tc.psum_pool(name="ps_y", bufs=2))
+        ps_s = ctx.enter_context(tc.psum_pool(name="ps_s", bufs=4))
+
+        offsets = held.tile([P, S // 16], U16, name="offsets")
+        nc.sync.dma_start(offsets[:], offs)
+
+        x_raw = held.tile([P, PACK, T], F32, name="x_raw")
+        x_rows = xT.rearrange("(p j) t -> p j t", j=PACK)
+        for j in range(PACK):
+            nc.sync.dma_start(out=x_raw[:, j, :], in_=x_rows[:, j, :])
+
+        z = [held.tile([P, T], F32, name=f"z{b}") for b in range(N // P)]
+        for b in range(N // P):
+            nc.vector.memset(z[b][:], 0.0)
+
+        gate_sb = held.tile([P, S], F32, name="gate_sb")
+        slot_codes = held.tile([P, S], U32, name="slot_codes", align_bytes=64)
+        slot_scales = held.tile([P, S], U8, name="slot_scales", align_bytes=64)
+        tok_codes = held.tile([P, T], U32, name="tok_codes", align_bytes=64)
+        tok_scales = held.tile([P, T], U8, name="tok_scales", align_bytes=64)
+        hs_codes = held.tile([P, T], U32, name="hs_codes", align_bytes=64)
+        hs_scales = held.tile([P, T], U8, name="hs_scales", align_bytes=64)
+
+        def copy_on(engine, dst, src):
+            if engine == "S":
+                nc.scalar.copy(out=dst, in_=src)
+            elif engine == "G":
+                nc.gpsimd.tensor_scalar(out=dst, in0=src, scalar1=1.0, scalar2=0.0, op0=MULT, op1=ADD)
+            else:
+                nc.vector.tensor_copy(out=dst, in_=src)
+
+        def load(w, e):
+            raw = rawp.tile([P, PACK, 512], F32, name="raw")
+            nc.sync.dma_start(out=raw[:], in_=w[e].rearrange("(p j) c -> p j c", j=PACK))
+            return raw
+
+        def interleave(raw, permute, shares):
+            wb = wbp.tile([P, PACK * 512], BF16, name="wb", align_bytes=64)
+            if permute:
+                dst = wb[:].rearrange("p (t m j) -> p m j t", t=PACK, j=PACK)
+                src = raw[:].rearrange("p j (m t) -> p m j t", t=PACK)
+            else:
+                dst = wb[:].rearrange("p (m i j) -> p m j i", i=4, j=PACK)
+                src = raw[:].rearrange("p j (m i) -> p m j i", i=4)
+            for engine, a, b in shares:
+                copy_on(engine, dst[:, a:b], src[:, a:b])
+            return wb
+
+        def quantize(wb, pool=wcp, name="wc"):
+            codes = pool.tile([P, 512], U32, name=name, align_bytes=64)
+            scales = pool.tile([P, 512], U8, name=name + "_s", align_bytes=64)
+            nc.vector.quantize_mx(out=codes[:].bitcast(FP8X4), scales=scales[:], in_=wb[:])
+            return codes, scales
+
+        def mx(dst, w, cols, x_codes, x_scales, xcols):
+            nc.tensor.matmul_mx(
+                out=dst,
+                lhsT=w[0][:, cols].bitcast(FP8X4),
+                lhsT_scale=w[1][:, cols],
+                rhs=x_codes[:, xcols].bitcast(FP8X4),
+                rhs_scale=x_scales[:, xcols],
+                start=True,
+                stop=True,
+            )
+
+        W1_SHARES = [("S", 0, 96), ("G", 96, 128)]
+        W2_SHARES = [("G", 0, 32), ("G", 32, 64), ("G", 64, 96), ("G", 96, 128)]
+
+        g4 = []
+        for h in range(2):
+            g4_tile = two.tile([P, PACK, HALF], F32, name="g4")
+            g4.append(g4_tile)
+        for j in range(PACK):
+            for h in range(2):
+                o = offsets[:, h * (HALF // 16) : (h + 1) * (HALF // 16)]
+                nc.vector.tensor_copy(g4[h][:, j, :], x_raw[:, j, :].indirect(o))
+
+        order = [("1", 0), ("2", 0), ("g", 0), ("1", 1), ("2", 1), ("1", E), ("1", 2), ("2", 2), ("1", 3), ("2", 3),
+                 ("2", E), ("1", 4), ("2", 4), ("1", 5), ("2", 5), ("1", 6), ("2", 6), ("1", 7), ("2", 7)]
+        raws = {}
+        bfs = {}
+        pos = [0]
+
+        def advance(n):
+            for _ in range(n):
+                if pos[0] < len(order):
+                    kind, e = order[pos[0]]
+                    pos[0] += 1
+                    if kind == "g":
+                        nc.sync.dma_start(out=gate_sb[:], in_=gate[0:P, :])
+                        kind, e = order[pos[0]]
+                        pos[0] += 1
+                    raws[kind, e] = load(w1 if kind == "1" else w2, e)
+
+        def prepare(kind, e):
+            bfs[kind, e] = interleave(raws[kind, e], kind == "1", W1_SHARES if kind == "1" else W2_SHARES)
+
+        advance(6)
+
+        for h in range(2):
+            xb = two.tile([P, PACK * HALF], BF16, name="xb", align_bytes=64)
+            dst = xb[:].rearrange("p (m i j) -> p m j i", i=4, j=PACK)
+            src = g4[h][:].rearrange("p j (m i) -> p m j i", i=4)
+            copy_on("S", dst[:, 0:64], src[:, 0:64])
+            copy_on("G", dst[:, 64:96], src[:, 64:96])
+            copy_on("G", dst[:, 96:128], src[:, 96:128])
+            cols = slice(h * HALF, (h + 1) * HALF)
+            nc.vector.quantize_mx(out=slot_codes[:, cols].bitcast(FP8X4), scales=slot_scales[:, cols], in_=xb[:])
+
+        prepare("1", 0)
+        prepare("2", 0)
+
+        shared = {}
+
+        def shared_piece(i):
+            t0 = i * PIECE
+            cols = slice(t0, t0 + PIECE)
+            tb = two.tile([P, PACK * PIECE], BF16, name="tb", align_bytes=64)
+            dst = tb[:].rearrange("p (m i j) -> p m j i", i=4, j=PACK)
+            src = x_raw[:, :, cols].rearrange("p j (m i) -> p m j i", i=4)
+            copy_on("G", dst[:, 0:32], src[:, 0:32])
+            copy_on("G", dst[:, 32:64], src[:, 32:64])
+            nc.vector.quantize_mx(out=tok_codes[:, cols].bitcast(FP8X4), scales=tok_scales[:, cols], in_=tb[:])
+            rs = two.tile([P, PACK, PIECE], F32, name="rs")
+            for a in range(2):
+                bank = ps_s.tile([P, 2, PIECE], F32, name="bank_s")
+                for u in range(2):
+                    t = 2 * a + u
+                    mx(bank[:, u, :], shared["1"], slice(t * P, (t + 1) * P), tok_codes, tok_scales, cols)
+                nc.scalar.activation(rs[:, 2 * a : 2 * a + 2, :], bank[:], RELU)
+            hsb = two.tile([P, PACK * PIECE], BF16, name="hsb", align_bytes=64)
+            nc.scalar.activation(
+                hsb[:].rearrange("p (m i t) -> p m t i", i=4, t=PACK),
+                rs[:].rearrange("p t (m i) -> p m t i", i=4),
+                SQUARE,
+            )
+            nc.vector.quantize_mx(out=hs_codes[:, cols].bitcast(FP8X4), scales=hs_scales[:, cols], in_=hsb[:])
+
+        pending = []
+        done = [0]
+
+        def scatter(n):
+            for _ in range(n):
+                if done[0] < len(pending):
+                    pair, b, values = pending[done[0]]
+                    done[0] += 1
+                    o = offsets[:, pair * 16 : (pair + 1) * 16]
+                    nc.vector.tensor_copy(z[b][:].indirect(o), values[:, b, :])
+
+        yg = None
+        for e in range(E):
+            w1q = quantize(bfs["1", e])
+            slots = slice(e * C, (e + 1) * C)
+            bank_a = ps_a.tile([P, PACK, C], F32, name="bank_a")
+            for t in range(PACK):
+                mx(bank_a[:, t, :], w1q, slice(t * P, (t + 1) * P), slot_codes, slot_scales, slots)
+            r = three.tile([P, PACK, C], F32, name="r")
+            nc.scalar.activation(r[:], bank_a[:], RELU)
+            hb = three.tile([P, PACK * C], BF16, name="hb", align_bytes=64)
+            nc.scalar.activation(
+                hb[:].rearrange("p (m i t) -> p m t i", i=4, t=PACK),
+                r[:].rearrange("p t (m i) -> p m t i", i=4),
+                SQUARE,
+            )
+            scatter(1)
+            advance(2)
+            if e == 1:
+                advance(1)
+                bfs["1", E] = interleave(raws["1", E], True, W1_SHARES)
+                shared["1"] = quantize(bfs["1", E], held, "ws1")
+            if e == 4:
+                advance(1)
+                bfs["2", E] = interleave(raws["2", E], False, W2_SHARES)
+                shared["2"] = quantize(bfs["2", E], held, "ws2")
+            if e + 1 < E:
+                prepare("1", e + 1)
+                prepare("2", e + 1)
+            w2q = quantize(bfs["2", e])
+            hc = three.tile([P, C], U32, name="hc", align_bytes=64)
+            hc_s = three.tile([P, C], U8, name="hc_s", align_bytes=64)
+            nc.vector.quantize_mx(out=hc[:].bitcast(FP8X4), scales=hc_s[:], in_=hb[:])
+            bank_y = ps_y.tile([P, N // P, C], F32, name="bank_y")
+            for b in range(N // P):
+                mx(bank_y[:, b, :], w2q, slice(b * P, (b + 1) * P), hc, hc_s, slice(0, C))
+            scatter(1)
+            if e % 2 == 0:
+                yg = two.tile([P, N // P, 2 * C], F32, name="yg")
+            half = slice((e % 2) * C, (e % 2 + 1) * C)
+            nc.vector.tensor_tensor(
+                out=yg[:, :, half],
+                in0=bank_y[:],
+                in1=gate_sb[:, slots].unsqueeze(1).to_broadcast([P, N // P, C]),
+                op=MULT,
+            )
+            if e % 2 == 1:
+                for b in range(N // P):
+                    pending.append((e // 2, b, yg))
+            if e >= 2:
+                shared_piece(e - 2)
+
+        for b in range(N // P):
+            scatter(1)
+            for c in range(T // CHUNK):
+                cols = slice(c * CHUNK, (c + 1) * CHUNK)
+                bank = ps_s.tile([P, CHUNK], F32, name="bank_s")
+                mx(bank[:], shared["2"], slice(b * P, (b + 1) * P), hs_codes, hs_scales, cols)
+                o_sb = outp.tile([P, CHUNK], F32, name="o_sb")
+                nc.vector.tensor_tensor(out=o_sb[:], in0=bank[:], in1=z[b][:, cols], op=ADD)
+                nc.sync.dma_start(out=out[b * P : (b + 1) * P, cols], in_=o_sb[:])

@@ -9,6 +9,7 @@ BYTES = 4 * (K * T + (E + 1) * (K * H + H * N) + S + N * T) + 2 * 128 * (S // 16
 
 F32 = mybir.dt.float32
 BF16 = mybir.dt.bfloat16
+I32 = mybir.dt.int32
 U32 = mybir.dt.uint32
 U16 = mybir.dt.uint16
 U8 = mybir.dt.uint8
@@ -16,41 +17,38 @@ FP8X4 = mybir.dt.float8_e4m3fn_x4
 ADD, MULT = mybir.AluOpType.add, mybir.AluOpType.mult
 RELU = mybir.ActivationFunctionType.Relu
 SQUARE = mybir.ActivationFunctionType.Square
+COPY = mybir.ActivationFunctionType.Copy
 
 P = 128
 PACK = 4
-HALF = 512
-PIECE = 256
+WIDTH = 512
 CHUNK = 512
+PAIR = 2 * C
+HALF = S // 2
+BLOCKS = N // P
+PAIRS = E // 2
+EARLY_SPLIT = 88
 
 
 def tile_moe_shr_mlp_relu2_kernel(tc, xT, w1, w2, gate, offs, out):
     nc = tc.nc
     with ExitStack() as ctx:
         held = ctx.enter_context(tc.tile_pool(name="held", bufs=1))
-        rawp = ctx.enter_context(tc.tile_pool(name="rawp", bufs=7))
-        wbp = ctx.enter_context(tc.tile_pool(name="wbp", bufs=4))
-        wcp = ctx.enter_context(tc.tile_pool(name="wcp", bufs=6))
+        rawp = ctx.enter_context(tc.tile_pool(name="rawp", bufs=8))
         two = ctx.enter_context(tc.tile_pool(name="two", bufs=2))
         three = ctx.enter_context(tc.tile_pool(name="three", bufs=3))
-        outp = ctx.enter_context(tc.tile_pool(name="outp", bufs=4))
-        ps_a = ctx.enter_context(tc.psum_pool(name="ps_a", bufs=2))
+        ps_a = ctx.enter_context(tc.psum_pool(name="ps_a", bufs=6))
         ps_y = ctx.enter_context(tc.psum_pool(name="ps_y", bufs=2))
-        ps_s = ctx.enter_context(tc.psum_pool(name="ps_s", bufs=4))
 
         offsets = held.tile([P, S // 16], U16, name="offsets")
         nc.sync.dma_start(offsets[:], offs)
 
-        x_raw = held.tile([P, PACK, T], F32, name="x_raw")
-        x_rows = xT.rearrange("(p j) t -> p j t", j=PACK)
-        for j in range(PACK):
-            nc.sync.dma_start(out=x_raw[:, j, :], in_=x_rows[:, j, :])
-
-        z = [held.tile([P, T], F32, name=f"z{b}") for b in range(N // P)]
-        for b in range(N // P):
+        z = [held.tile([P, T], F32, name=f"z{b}") for b in range(BLOCKS)]
+        for b in range(BLOCKS):
             nc.vector.memset(z[b][:], 0.0)
 
         gate_sb = held.tile([P, S], F32, name="gate_sb")
+        planes = held.tile([P, 2 * T], U32, name="planes")
         slot_codes = held.tile([P, S], U32, name="slot_codes", align_bytes=64)
         slot_scales = held.tile([P, S], U8, name="slot_scales", align_bytes=64)
         tok_codes = held.tile([P, T], U32, name="tok_codes", align_bytes=64)
@@ -58,189 +56,208 @@ def tile_moe_shr_mlp_relu2_kernel(tc, xT, w1, w2, gate, offs, out):
         hs_codes = held.tile([P, T], U32, name="hs_codes", align_bytes=64)
         hs_scales = held.tile([P, T], U8, name="hs_scales", align_bytes=64)
 
-        def copy_on(engine, dst, src):
-            if engine == "S":
-                nc.scalar.copy(out=dst, in_=src)
-            elif engine == "G":
-                nc.gpsimd.tensor_scalar(out=dst, in0=src, scalar1=1.0, scalar2=0.0, op0=MULT, op1=ADD)
-            else:
-                nc.vector.tensor_copy(out=dst, in_=src)
+        sources = {("x", c): xT[:, c * CHUNK : (c + 1) * CHUNK] for c in range(T // CHUNK)}
+        for e in range(E + 1):
+            sources["w1", e] = w1[e]
+            sources["w2", e] = w2[e]
+        order = [("x", 0), ("w1", E), ("x", 1), ("x", 2)]
+        order.extend([("w1", 0), ("w1", 1)])
+        for q in range(PAIRS):
+            order.extend([("w1", 2 * q + 2), ("w1", 2 * q + 3)] if q + 1 < PAIRS else [("w2", E)])
+            order.extend([("w2", 2 * q), ("w2", 2 * q + 1)])
+        raws = {}
 
-        def load(w, e):
-            raw = rawp.tile([P, PACK, 512], F32, name="raw")
-            nc.sync.dma_start(out=raw[:], in_=w[e].rearrange("(p j) c -> p j c", j=PACK))
-            return raw
+        def load_next():
+            if len(raws) < len(order):
+                key = order[len(raws)]
+                raw = rawp.tile([P, PACK, WIDTH], F32, name="raw")
+                nc.sync.dma_start(out=raw[:], in_=sources[key].rearrange("(p j) c -> p j c", j=PACK))
+                raws[key] = raw
+                if key == ("w1", 3):
+                    nc.sync.dma_start(out=gate_sb[:], in_=gate[0:P, :])
 
-        def interleave(raw, permute, shares):
-            wb = wbp.tile([P, PACK * 512], BF16, name="wb", align_bytes=64)
-            if permute:
-                dst = wb[:].rearrange("p (t m j) -> p m j t", t=PACK, j=PACK)
+        def cast(key, grouped, on_vector):
+            raw = raws[key]
+            if key[0] == "w1":
+                dst = grouped.rearrange("p (t m j) -> p m j t", t=PACK, j=PACK)
                 src = raw[:].rearrange("p j (m t) -> p m j t", t=PACK)
             else:
-                dst = wb[:].rearrange("p (m i j) -> p m j i", i=4, j=PACK)
+                dst = grouped.rearrange("p (m i j) -> p m j i", i=4, j=PACK)
                 src = raw[:].rearrange("p j (m i) -> p m j i", i=4)
-            for engine, a, b in shares:
-                copy_on(engine, dst[:, a:b], src[:, a:b])
-            return wb
+            if on_vector > 0:
+                nc.vector.tensor_copy(out=dst[:, :on_vector], in_=src[:, :on_vector])
+            if on_vector < P:
+                nc.scalar.copy(out=dst[:, on_vector:], in_=src[:, on_vector:])
+            load_next()
 
-        def quantize(wb, pool=wcp, name="wc"):
-            codes = pool.tile([P, 512], U32, name=name, align_bytes=64)
-            scales = pool.tile([P, 512], U8, name=name + "_s", align_bytes=64)
-            nc.vector.quantize_mx(out=codes[:].bitcast(FP8X4), scales=scales[:], in_=wb[:])
-            return codes, scales
+        def quantize(codes, scales, grouped):
+            nc.vector.quantize_mx(out=codes.bitcast(FP8X4), scales=scales, in_=grouped)
 
-        def mx(dst, w, cols, x_codes, x_scales, xcols):
+        def mx(dst, w, wcols, x, xcols):
             nc.tensor.matmul_mx(
                 out=dst,
-                lhsT=w[0][:, cols].bitcast(FP8X4),
-                lhsT_scale=w[1][:, cols],
-                rhs=x_codes[:, xcols].bitcast(FP8X4),
-                rhs_scale=x_scales[:, xcols],
+                lhsT=w[0][:, wcols].bitcast(FP8X4),
+                lhsT_scale=w[1][:, wcols],
+                rhs=x[0][:, xcols].bitcast(FP8X4),
+                rhs_scale=x[1][:, xcols],
                 start=True,
                 stop=True,
             )
 
-        W1_SHARES = [("S", 0, 96), ("G", 96, 128)]
-        W2_SHARES = [("G", 0, 32), ("G", 32, 64), ("G", 64, 96), ("G", 96, 128)]
-
-        g4 = []
-        for h in range(2):
-            g4_tile = two.tile([P, PACK, HALF], F32, name="g4")
-            g4.append(g4_tile)
-        for j in range(PACK):
-            for h in range(2):
-                o = offsets[:, h * (HALF // 16) : (h + 1) * (HALF // 16)]
-                nc.vector.tensor_copy(g4[h][:, j, :], x_raw[:, j, :].indirect(o))
-
-        order = [("1", 0), ("2", 0), ("g", 0), ("1", 1), ("2", 1), ("1", E), ("1", 2), ("2", 2), ("1", 3), ("2", 3),
-                 ("2", E), ("1", 4), ("2", 4), ("1", 5), ("2", 5), ("1", 6), ("2", 6), ("1", 7), ("2", 7)]
-        raws = {}
-        bfs = {}
-        pos = [0]
-
-        def advance(n):
-            for _ in range(n):
-                if pos[0] < len(order):
-                    kind, e = order[pos[0]]
-                    pos[0] += 1
-                    if kind == "g":
-                        nc.sync.dma_start(out=gate_sb[:], in_=gate[0:P, :])
-                        kind, e = order[pos[0]]
-                        pos[0] += 1
-                    raws[kind, e] = load(w1 if kind == "1" else w2, e)
-
-        def prepare(kind, e):
-            bfs[kind, e] = interleave(raws[kind, e], kind == "1", W1_SHARES if kind == "1" else W2_SHARES)
-
-        advance(6)
-
-        for h in range(2):
-            xb = two.tile([P, PACK * HALF], BF16, name="xb", align_bytes=64)
-            dst = xb[:].rearrange("p (m i j) -> p m j i", i=4, j=PACK)
-            src = g4[h][:].rearrange("p j (m i) -> p m j i", i=4)
-            copy_on("S", dst[:, 0:64], src[:, 0:64])
-            copy_on("G", dst[:, 64:96], src[:, 64:96])
-            copy_on("G", dst[:, 96:128], src[:, 96:128])
-            cols = slice(h * HALF, (h + 1) * HALF)
-            nc.vector.quantize_mx(out=slot_codes[:, cols].bitcast(FP8X4), scales=slot_scales[:, cols], in_=xb[:])
-
-        prepare("1", 0)
-        prepare("2", 0)
-
-        shared = {}
-
-        def shared_piece(i):
-            t0 = i * PIECE
-            cols = slice(t0, t0 + PIECE)
-            tb = two.tile([P, PACK * PIECE], BF16, name="tb", align_bytes=64)
-            dst = tb[:].rearrange("p (m i j) -> p m j i", i=4, j=PACK)
-            src = x_raw[:, :, cols].rearrange("p j (m i) -> p m j i", i=4)
-            copy_on("G", dst[:, 0:32], src[:, 0:32])
-            copy_on("G", dst[:, 32:64], src[:, 32:64])
-            nc.vector.quantize_mx(out=tok_codes[:, cols].bitcast(FP8X4), scales=tok_scales[:, cols], in_=tb[:])
-            rs = two.tile([P, PACK, PIECE], F32, name="rs")
-            for a in range(2):
-                bank = ps_s.tile([P, 2, PIECE], F32, name="bank_s")
-                for u in range(2):
-                    t = 2 * a + u
-                    mx(bank[:, u, :], shared["1"], slice(t * P, (t + 1) * P), tok_codes, tok_scales, cols)
-                nc.scalar.activation(rs[:, 2 * a : 2 * a + 2, :], bank[:], RELU)
-            hsb = two.tile([P, PACK * PIECE], BF16, name="hsb", align_bytes=64)
-            nc.scalar.activation(
-                hsb[:].rearrange("p (m i t) -> p m t i", i=4, t=PACK),
-                rs[:].rearrange("p t (m i) -> p m t i", i=4),
-                SQUARE,
-            )
-            nc.vector.quantize_mx(out=hs_codes[:, cols].bitcast(FP8X4), scales=hs_scales[:, cols], in_=hsb[:])
-
-        pending = []
-        done = [0]
-
-        def scatter(n):
-            for _ in range(n):
-                if done[0] < len(pending):
-                    pair, b, values = pending[done[0]]
-                    done[0] += 1
-                    o = offsets[:, pair * 16 : (pair + 1) * 16]
-                    nc.vector.tensor_copy(z[b][:].indirect(o), values[:, b, :])
-
-        yg = None
-        for e in range(E):
-            w1q = quantize(bfs["1", e])
-            slots = slice(e * C, (e + 1) * C)
-            bank_a = ps_a.tile([P, PACK, C], F32, name="bank_a")
+        def first_layer(w, w0, x, x0, relu_out):
+            bank = ps_a.tile([P, PACK, C], F32, name="bank_a")
             for t in range(PACK):
-                mx(bank_a[:, t, :], w1q, slice(t * P, (t + 1) * P), slot_codes, slot_scales, slots)
-            r = three.tile([P, PACK, C], F32, name="r")
-            nc.scalar.activation(r[:], bank_a[:], RELU)
-            hb = three.tile([P, PACK * C], BF16, name="hb", align_bytes=64)
-            nc.scalar.activation(
-                hb[:].rearrange("p (m i t) -> p m t i", i=4, t=PACK),
-                r[:].rearrange("p t (m i) -> p m t i", i=4),
-                SQUARE,
-            )
-            scatter(1)
-            advance(2)
-            if e == 1:
-                advance(1)
-                bfs["1", E] = interleave(raws["1", E], True, W1_SHARES)
-                shared["1"] = quantize(bfs["1", E], held, "ws1")
-            if e == 4:
-                advance(1)
-                bfs["2", E] = interleave(raws["2", E], False, W2_SHARES)
-                shared["2"] = quantize(bfs["2", E], held, "ws2")
-            if e + 1 < E:
-                prepare("1", e + 1)
-                prepare("2", e + 1)
-            w2q = quantize(bfs["2", e])
-            hc = three.tile([P, C], U32, name="hc", align_bytes=64)
-            hc_s = three.tile([P, C], U8, name="hc_s", align_bytes=64)
-            nc.vector.quantize_mx(out=hc[:].bitcast(FP8X4), scales=hc_s[:], in_=hb[:])
-            bank_y = ps_y.tile([P, N // P, C], F32, name="bank_y")
-            for b in range(N // P):
-                mx(bank_y[:, b, :], w2q, slice(b * P, (b + 1) * P), hc, hc_s, slice(0, C))
-            scatter(1)
-            if e % 2 == 0:
-                yg = two.tile([P, N // P, 2 * C], F32, name="yg")
-            half = slice((e % 2) * C, (e % 2 + 1) * C)
-            nc.vector.tensor_tensor(
-                out=yg[:, :, half],
-                in0=bank_y[:],
-                in1=gate_sb[:, slots].unsqueeze(1).to_broadcast([P, N // P, C]),
-                op=MULT,
-            )
-            if e % 2 == 1:
-                for b in range(N // P):
-                    pending.append((e // 2, b, yg))
-            if e >= 2:
-                shared_piece(e - 2)
+                mx(bank[:, t, :], w, slice(w0 + t * P, w0 + (t + 1) * P), x, slice(x0, x0 + C))
+            nc.scalar.activation(relu_out.rearrange("p (c t) -> p c t", t=PACK), bank[:].rearrange("p t c -> p c t"), RELU)
 
-        for b in range(N // P):
-            scatter(1)
+        slots = (slot_codes, slot_scales)
+        tokens = (tok_codes, tok_scales)
+        hidden_s = (hs_codes, hs_scales)
+        ws1 = (held.tile([P, WIDTH], U32, name="ws1c", align_bytes=64), held.tile([P, WIDTH], U8, name="ws1s", align_bytes=64))
+        ws2 = (held.tile([P, WIDTH], U32, name="ws2c", align_bytes=64), held.tile([P, WIDTH], U8, name="ws2s", align_bytes=64))
+
+        for n in range(8):
+            load_next()
+
+        def tokens_in(c, on_vector):
+            cols = slice(c * CHUNK, (c + 1) * CHUNK)
+            xb = two.tile([P, PACK * CHUNK], BF16, name="xb", align_bytes=64)
+            cast(("x", c), xb[:], on_vector)
+            nc.vector.tensor_copy(
+                out=planes[:].bitcast(I32).rearrange("p (u t) -> p u t", u=2)[:, :, cols],
+                in_=xb[:].bitcast(I32).rearrange("p (t u) -> p u t", u=2),
+            )
+            quantize(tok_codes[:, cols], tok_scales[:, cols], xb[:])
+
+        hsb = {}
+
+        def shared_first(c):
+            hsb[c] = three.tile([P, PACK * CHUNK], BF16, name="hsb", align_bytes=64)
+            for a in range(2):
+                r = two.tile([P, PACK * PAIR], F32, name="r")
+                for u in range(2):
+                    first_layer(ws1, 0, tokens, c * CHUNK + a * PAIR + u * C, r[:, u * PACK * C : (u + 1) * PACK * C])
+                nc.scalar.activation(hsb[c][:, a * PACK * PAIR : (a + 1) * PACK * PAIR], r[:], SQUARE)
+
+        def shared_hidden(c):
+            cols = slice(c * CHUNK, (c + 1) * CHUNK)
+            quantize(hs_codes[:, cols], hs_scales[:, cols], hsb[c][:])
+
+        picked = {}
+
+        def gather(h):
+            picked[h] = two.tile([P, 2 * HALF], U32, name="picked")
+            o = offsets[:, h * (HALF // 16) : (h + 1) * (HALF // 16)]
+            for u in range(2):
+                nc.vector.tensor_copy(picked[h][:, u * HALF : (u + 1) * HALF], planes[:, u * T : (u + 1) * T].indirect(o))
+
+        def weave(h):
+            sb = two.tile([P, PACK * HALF], BF16, name="xb", align_bytes=64)
+            nc.vector.tensor_copy(
+                out=sb[:].bitcast(I32).rearrange("p (s u) -> p s u", u=2),
+                in_=picked[h][:].bitcast(I32).rearrange("p (u s) -> p s u", u=2),
+            )
+            return sb
+
+        grouped = {}
+        codes = {}
+        hb = {}
+        hq = {}
+        yg = {}
+
+        def cast_w(kind, q, u, on_vector):
+            if u == 0:
+                grouped[kind, q] = three.tile([P, 2 * PACK * WIDTH], BF16, name="wb", align_bytes=64)
+            cast((kind, 2 * q + u), grouped[kind, q][:, u * PACK * WIDTH : (u + 1) * PACK * WIDTH], on_vector)
+
+        def quantize_w(kind, q):
+            wc = two.tile([P, 2 * WIDTH], U32, name=kind + "c", align_bytes=64)
+            ws = two.tile([P, 2 * WIDTH], U8, name=kind + "s", align_bytes=64)
+            codes[kind, q] = (wc, ws)
+            quantize(wc[:], ws[:], grouped[kind, q][:])
+
+        def routed_first(q):
+            r = two.tile([P, PACK * PAIR], F32, name="r")
+            for u in range(2):
+                first_layer(codes["w1", q], u * WIDTH, slots, q * PAIR + u * C, r[:, u * PACK * C : (u + 1) * PACK * C])
+            hb[q] = two.tile([P, PACK * PAIR], BF16, name="hb", align_bytes=64)
+            nc.scalar.activation(hb[q][:], r[:], SQUARE)
+
+        def routed_hidden(q):
+            hc = held.tile([P, PAIR], U32, name="hc", align_bytes=64)
+            hs = held.tile([P, PAIR], U8, name="hs", align_bytes=64)
+            hq[q] = (hc, hs)
+            quantize(hc[:], hs[:], hb[q][:])
+
+        def routed_second(q):
+            yg[q] = two.tile([P, BLOCKS, PAIR], F32, name="yg")
+            for u in range(2):
+                bank = ps_y.tile([P, BLOCKS, C], F32, name="bank_y")
+                for b in range(BLOCKS):
+                    mx(bank[:, b, :], codes["w2", q], slice(u * WIDTH + b * P, u * WIDTH + (b + 1) * P), hq[q], slice(u * C, (u + 1) * C))
+                s0 = q * PAIR + u * C
+                nc.vector.tensor_tensor(
+                    out=yg[q][:, :, u * C : (u + 1) * C],
+                    in0=bank[:],
+                    in1=gate_sb[:, s0 : s0 + C].unsqueeze(1).to_broadcast([P, BLOCKS, C]),
+                    op=MULT,
+                )
+
+        def scatter(q, b):
+            o = offsets[:, q * (PAIR // 16) : (q + 1) * (PAIR // 16)]
+            nc.scalar.activation(z[b][:].indirect(o), yg[q][:, b, :], COPY)
+
+        tokens_in(0, EARLY_SPLIT)
+        wsb = two.tile([P, PACK * WIDTH], BF16, name="xb", align_bytes=64)
+        cast(("w1", E), wsb[:], EARLY_SPLIT)
+        quantize(ws1[0][:], ws1[1][:], wsb[:])
+        tokens_in(1, 0)
+        shared_first(0)
+        tokens_in(2, P)
+        cast_w("w1", 0, 0, 0)
+        gather(0)
+        sb = weave(0)
+        cast_w("w1", 0, 1, P)
+        quantize(slot_codes[:, :HALF], slot_scales[:, :HALF], sb[:])
+        quantize_w("w1", 0)
+        shared_first(1)
+        routed_first(0)
+
+        for q in range(PAIRS):
+            if q + 1 < PAIRS:
+                cast_w("w1", q + 1, 0, 0 if q == 0 else P)
+                cast_w("w1", q + 1, 1, P)
+            else:
+                wsb = two.tile([P, PACK * WIDTH], BF16, name="xb", align_bytes=64)
+                cast(("w2", E), wsb[:], P)
+            routed_hidden(q)
+            if q == 0:
+                shared_first(2)
+            if q + 1 < PAIRS:
+                quantize_w("w1", q + 1)
+                routed_first(q + 1)
+            else:
+                quantize(ws2[0][:], ws2[1][:], wsb[:])
+            cast_w("w2", q, 0, P)
+            cast_w("w2", q, 1, P)
+            if q < T // CHUNK:
+                shared_hidden(q)
+            quantize_w("w2", q)
+            if q == 0:
+                gather(1)
+            routed_second(q)
+            if q == 0:
+                sb = weave(1)
+                quantize(slot_codes[:, HALF:], slot_scales[:, HALF:], sb[:])
+            if q + 1 < PAIRS:
+                for b in range(BLOCKS):
+                    scatter(q, b)
+
+        for b in range(BLOCKS):
+            scatter(PAIRS - 1, b)
             for c in range(T // CHUNK):
                 cols = slice(c * CHUNK, (c + 1) * CHUNK)
-                bank = ps_s.tile([P, CHUNK], F32, name="bank_s")
-                mx(bank[:], shared["2"], slice(b * P, (b + 1) * P), hs_codes, hs_scales, cols)
-                o_sb = outp.tile([P, CHUNK], F32, name="o_sb")
-                nc.vector.tensor_tensor(out=o_sb[:], in0=bank[:], in1=z[b][:, cols], op=ADD)
-                nc.sync.dma_start(out=out[b * P : (b + 1) * P, cols], in_=o_sb[:])
+                bank = ps_a.tile([P, CHUNK], F32, name="bank_a")
+                mx(bank[:], ws2, slice(b * P, (b + 1) * P), hidden_s, cols)
+                nc.vector.tensor_tensor(out=z[b][:, cols], in0=bank[:], in1=z[b][:, cols], op=ADD)
+                nc.sync.dma_start(out=out[b * P : (b + 1) * P, cols], in_=z[b][:, cols])

@@ -27,7 +27,7 @@ PAIR = 2 * C
 HALF = S // 2
 BLOCKS = N // P
 PAIRS = E // 2
-EARLY_SPLIT = 88
+EARLY_SPLIT = 40
 
 
 def tile_moe_shr_mlp_relu2_kernel(tc, xT, w1, w2, gate, offs, out):
@@ -41,11 +41,11 @@ def tile_moe_shr_mlp_relu2_kernel(tc, xT, w1, w2, gate, offs, out):
         ps_y = ctx.enter_context(tc.psum_pool(name="ps_y", bufs=2))
 
         offsets = held.tile([P, S // 16], U16, name="offsets")
-        nc.sync.dma_start(offsets[:], offs)
 
         z = [held.tile([P, T], F32, name=f"z{b}") for b in range(BLOCKS)]
-        for b in range(BLOCKS):
+        for b in range(BLOCKS - 1):
             nc.vector.memset(z[b][:], 0.0)
+        nc.gpsimd.memset(z[BLOCKS - 1][:], 0.0)
 
         gate_sb = held.tile([P, S], F32, name="gate_sb")
         planes = held.tile([P, 2 * T], U32, name="planes")
@@ -60,7 +60,10 @@ def tile_moe_shr_mlp_relu2_kernel(tc, xT, w1, w2, gate, offs, out):
         for e in range(E + 1):
             sources["w1", e] = w1[e]
             sources["w2", e] = w2[e]
-        order = [("x", 0), ("w1", E), ("x", 1), ("x", 2)]
+        for h in range(2):
+            sources["w1", E, h] = w1[E][:, h * PAIR : (h + 1) * PAIR]
+            sources["x", 0, h] = xT[:, h * PAIR : (h + 1) * PAIR]
+        order = [("w1", E, 0), ("w1", E, 1), ("x", 0, 0), ("x", 0, 1), ("x", 1), ("x", 2)]
         order.extend([("w1", 0), ("w1", 1)])
         for q in range(PAIRS):
             order.extend([("w1", 2 * q + 2), ("w1", 2 * q + 3)] if q + 1 < PAIRS else [("w2", E)])
@@ -70,23 +73,30 @@ def tile_moe_shr_mlp_relu2_kernel(tc, xT, w1, w2, gate, offs, out):
         def load_next():
             if len(raws) < len(order):
                 key = order[len(raws)]
-                raw = rawp.tile([P, PACK, WIDTH], F32, name="raw")
+                raw = rawp.tile([P, PACK, sources[key].shape[1]], F32, name="raw")
                 nc.sync.dma_start(out=raw[:], in_=sources[key].rearrange("(p j) c -> p j c", j=PACK))
                 raws[key] = raw
+                if key == ("x", 1):
+                    nc.sync.dma_start(offsets[:], offs)
                 if key == ("w1", 3):
                     nc.sync.dma_start(out=gate_sb[:], in_=gate[0:P, :])
 
         def cast(key, grouped, on_vector):
             raw = raws[key]
+            quads = raw.shape[2] // 4
+            first = key[2] * quads if len(key) == 3 else 0
             if key[0] == "w1":
                 dst = grouped.rearrange("p (t m j) -> p m j t", t=PACK, j=PACK)
-                src = raw[:].rearrange("p j (m t) -> p m j t", t=PACK)
             else:
-                dst = grouped.rearrange("p (m i j) -> p m j i", i=4, j=PACK)
+                dst = grouped.rearrange("p (m h i j) -> p m h j i", h=2, i=2, j=PACK)
+            dst = dst[:, first : first + quads]
+            if key[0] == "w1":
                 src = raw[:].rearrange("p j (m i) -> p m j i", i=4)
+            else:
+                src = raw[:].rearrange("p j (m h i) -> p m h j i", h=2, i=2)
             if on_vector > 0:
                 nc.vector.tensor_copy(out=dst[:, :on_vector], in_=src[:, :on_vector])
-            if on_vector < P:
+            if on_vector < quads:
                 nc.scalar.copy(out=dst[:, on_vector:], in_=src[:, on_vector:])
             load_next()
 
@@ -119,25 +129,28 @@ def tile_moe_shr_mlp_relu2_kernel(tc, xT, w1, w2, gate, offs, out):
         for n in range(8):
             load_next()
 
-        def tokens_in(c, on_vector):
-            cols = slice(c * CHUNK, (c + 1) * CHUNK)
-            xb = two.tile([P, PACK * CHUNK], BF16, name="xb", align_bytes=64)
-            cast(("x", c), xb[:], on_vector)
+        xb = {}
+
+        def split_planes(c):
             nc.vector.tensor_copy(
-                out=planes[:].bitcast(I32).rearrange("p (u t) -> p u t", u=2)[:, :, cols],
-                in_=xb[:].bitcast(I32).rearrange("p (t u) -> p u t", u=2),
+                out=planes[:].bitcast(I32).rearrange("p (u t) -> p u t", u=2)[:, :, c * CHUNK : (c + 1) * CHUNK],
+                in_=xb[c][:].bitcast(I32).rearrange("p (t u) -> p u t", u=2),
             )
-            quantize(tok_codes[:, cols], tok_scales[:, cols], xb[:])
+
+        def quantize_tokens(c, t0, t1):
+            cols = slice(c * CHUNK + t0, c * CHUNK + t1)
+            quantize(tok_codes[:, cols], tok_scales[:, cols], xb[c][:, PACK * t0 : PACK * t1])
 
         hsb = {}
 
-        def shared_first(c):
+        def shared_first(c, room=None):
             hsb[c] = three.tile([P, PACK * CHUNK], BF16, name="hsb", align_bytes=64)
             for a in range(2):
-                r = two.tile([P, PACK * PAIR], F32, name="r")
+                half = slice(a * PACK * PAIR, (a + 1) * PACK * PAIR)
+                r = two.tile([P, PACK * PAIR], F32, name="r")[:] if room is None else room[:, half]
                 for u in range(2):
                     first_layer(ws1, 0, tokens, c * CHUNK + a * PAIR + u * C, r[:, u * PACK * C : (u + 1) * PACK * C])
-                nc.scalar.activation(hsb[c][:, a * PACK * PAIR : (a + 1) * PACK * PAIR], r[:], SQUARE)
+                nc.scalar.activation(hsb[c][:, half], r, SQUARE)
 
         def shared_hidden(c):
             cols = slice(c * CHUNK, (c + 1) * CHUNK)
@@ -145,17 +158,17 @@ def tile_moe_shr_mlp_relu2_kernel(tc, xT, w1, w2, gate, offs, out):
 
         picked = {}
 
-        def gather(h):
-            picked[h] = two.tile([P, 2 * HALF], U32, name="picked")
+        def gather(h, room):
+            picked[h] = room
             o = offsets[:, h * (HALF // 16) : (h + 1) * (HALF // 16)]
             for u in range(2):
                 nc.vector.tensor_copy(picked[h][:, u * HALF : (u + 1) * HALF], planes[:, u * T : (u + 1) * T].indirect(o))
 
         def weave(h):
-            sb = two.tile([P, PACK * HALF], BF16, name="xb", align_bytes=64)
+            sb = three.tile([P, PACK * HALF], BF16, name="xb", align_bytes=64)
             nc.vector.tensor_copy(
                 out=sb[:].bitcast(I32).rearrange("p (s u) -> p s u", u=2),
-                in_=picked[h][:].bitcast(I32).rearrange("p (u s) -> p s u", u=2),
+                in_=picked[h].bitcast(I32).rearrange("p (u s) -> p s u", u=2),
             )
             return sb
 
@@ -191,15 +204,16 @@ def tile_moe_shr_mlp_relu2_kernel(tc, xT, w1, w2, gate, offs, out):
 
         def routed_second(q):
             yg[q] = two.tile([P, BLOCKS, PAIR], F32, name="yg")
-            for u in range(2):
-                bank = ps_y.tile([P, BLOCKS, C], F32, name="bank_y")
-                for b in range(BLOCKS):
-                    mx(bank[:, b, :], codes["w2", q], slice(u * WIDTH + b * P, u * WIDTH + (b + 1) * P), hq[q], slice(u * C, (u + 1) * C))
-                s0 = q * PAIR + u * C
+            for a in range(2):
+                bank = ps_y.tile([P, 2, PAIR], F32, name="bank_y")
+                for i in range(2):
+                    for u in range(2):
+                        w0 = u * WIDTH + (2 * a + i) * P
+                        mx(bank[:, i, u * C : (u + 1) * C], codes["w2", q], slice(w0, w0 + P), hq[q], slice(u * C, (u + 1) * C))
                 nc.vector.tensor_tensor(
-                    out=yg[q][:, :, u * C : (u + 1) * C],
+                    out=yg[q][:, 2 * a : 2 * a + 2, :],
                     in0=bank[:],
-                    in1=gate_sb[:, s0 : s0 + C].unsqueeze(1).to_broadcast([P, BLOCKS, C]),
+                    in1=gate_sb[:, q * PAIR : (q + 1) * PAIR].unsqueeze(1).to_broadcast([P, 2, PAIR]),
                     op=MULT,
                 )
 
@@ -207,15 +221,24 @@ def tile_moe_shr_mlp_relu2_kernel(tc, xT, w1, w2, gate, offs, out):
             o = offsets[:, q * (PAIR // 16) : (q + 1) * (PAIR // 16)]
             nc.scalar.activation(z[b][:].indirect(o), yg[q][:, b, :], COPY)
 
-        tokens_in(0, EARLY_SPLIT)
-        wsb = two.tile([P, PACK * WIDTH], BF16, name="xb", align_bytes=64)
-        cast(("w1", E), wsb[:], EARLY_SPLIT)
+        wsb = three.tile([P, PACK * WIDTH], BF16, name="xb", align_bytes=64)
+        cast(("w1", E, 0), wsb[:], 0)
+        cast(("w1", E, 1), wsb[:], P // 2)
         quantize(ws1[0][:], ws1[1][:], wsb[:])
-        tokens_in(1, 0)
+        xb[0] = three.tile([P, PACK * CHUNK], BF16, name="xb", align_bytes=64)
+        cast(("x", 0, 0), xb[0][:], EARLY_SPLIT)
+        quantize_tokens(0, 0, PAIR)
+        cast(("x", 0, 1), xb[0][:], 0)
+        quantize_tokens(0, PAIR, CHUNK)
         shared_first(0)
-        tokens_in(2, P)
+        split_planes(0)
+        for c in (1, 2):
+            xb[c] = three.tile([P, PACK * CHUNK], BF16, name="xb", align_bytes=64)
+            cast(("x", c), xb[c][:], P)
+            split_planes(c)
+            quantize_tokens(c, 0, CHUNK)
         cast_w("w1", 0, 0, 0)
-        gather(0)
+        gather(0, held.tile([P, 2 * HALF], U32, name="picked")[:])
         sb = weave(0)
         cast_w("w1", 0, 1, P)
         quantize(slot_codes[:, :HALF], slot_scales[:, :HALF], sb[:])
@@ -228,11 +251,11 @@ def tile_moe_shr_mlp_relu2_kernel(tc, xT, w1, w2, gate, offs, out):
                 cast_w("w1", q + 1, 0, 0 if q == 0 else P)
                 cast_w("w1", q + 1, 1, P)
             else:
-                wsb = two.tile([P, PACK * WIDTH], BF16, name="xb", align_bytes=64)
+                wsb = three.tile([P, PACK * WIDTH], BF16, name="xb", align_bytes=64)
                 cast(("w2", E), wsb[:], P)
             routed_hidden(q)
             if q == 0:
-                shared_first(2)
+                shared_first(2, grouped["w1", 0][:].bitcast(F32))
             if q + 1 < PAIRS:
                 quantize_w("w1", q + 1)
                 routed_first(q + 1)
@@ -243,10 +266,9 @@ def tile_moe_shr_mlp_relu2_kernel(tc, xT, w1, w2, gate, offs, out):
             if q < T // CHUNK:
                 shared_hidden(q)
             quantize_w("w2", q)
-            if q == 0:
-                gather(1)
             routed_second(q)
             if q == 0:
+                gather(1, grouped["w2", 0][:].bitcast(U32)[:, : 2 * HALF])
                 sb = weave(1)
                 quantize(slot_codes[:, HALF:], slot_scales[:, HALF:], sb[:])
             if q + 1 < PAIRS:

@@ -88,12 +88,9 @@ def tile_moe_shr_mlp_relu2_kernel(tc, xT, w1, w2, gate, offs, out):
             if key[0] == "w1":
                 dst = grouped.rearrange("p (t m j) -> p m j t", t=PACK, j=PACK)
             else:
-                dst = grouped.rearrange("p (m h i j) -> p m h j i", h=2, i=2, j=PACK)
+                dst = grouped.rearrange("p (m i j) -> p m j i", i=4, j=PACK)
             dst = dst[:, first : first + quads]
-            if key[0] == "w1":
-                src = raw[:].rearrange("p j (m i) -> p m j i", i=4)
-            else:
-                src = raw[:].rearrange("p j (m h i) -> p m h j i", h=2, i=2)
+            src = raw[:].rearrange("p j (m i) -> p m j i", i=4)
             if on_vector > 0:
                 nc.vector.tensor_copy(out=dst[:, :on_vector], in_=src[:, :on_vector])
             if on_vector < quads:
@@ -249,7 +246,7 @@ def tile_moe_shr_mlp_relu2_kernel(tc, xT, w1, w2, gate, offs, out):
         for q in range(PAIRS):
             if q + 1 < PAIRS:
                 cast_w("w1", q + 1, 0, 0 if q == 0 else P)
-                cast_w("w1", q + 1, 1, P)
+                cast_w("w1", q + 1, 1, P // 2 if q == 0 else P)
             else:
                 wsb = three.tile([P, PACK * WIDTH], BF16, name="xb", align_bytes=64)
                 cast(("w2", E), wsb[:], P)

@@ -27,6 +27,9 @@ PAIR = 2 * C
 HALF = S // 2
 BLOCKS = N // P
 PAIRS = E // 2
+QUADS = WIDTH // 4
+REGION = 2 * PACK * WIDTH * 4
+REGIONS = 4
 EARLY_SPLIT = 40
 
 
@@ -34,14 +37,13 @@ def tile_moe_shr_mlp_relu2_kernel(tc, xT, w1, w2, gate, offs, out):
     nc = tc.nc
     with ExitStack() as ctx:
         held = ctx.enter_context(tc.tile_pool(name="held", bufs=1))
-        rawp = ctx.enter_context(tc.tile_pool(name="rawp", bufs=8))
+        rawp = ctx.enter_context(tc.tile_pool(name="rawp", bufs=1))
         two = ctx.enter_context(tc.tile_pool(name="two", bufs=2))
         three = ctx.enter_context(tc.tile_pool(name="three", bufs=3))
         ps_a = ctx.enter_context(tc.psum_pool(name="ps_a", bufs=6))
         ps_y = ctx.enter_context(tc.psum_pool(name="ps_y", bufs=2))
 
         offsets = held.tile([P, S // 16], U16, name="offsets")
-
         z = [held.tile([P, T], F32, name=f"z{b}") for b in range(BLOCKS)]
         for b in range(BLOCKS - 1):
             nc.vector.memset(z[b][:], 0.0)
@@ -49,56 +51,58 @@ def tile_moe_shr_mlp_relu2_kernel(tc, xT, w1, w2, gate, offs, out):
 
         gate_sb = held.tile([P, S], F32, name="gate_sb")
         planes = held.tile([P, 2 * T], U32, name="planes")
-        slot_codes = held.tile([P, S], U32, name="slot_codes", align_bytes=64)
-        slot_scales = held.tile([P, S], U8, name="slot_scales", align_bytes=64)
-        tok_codes = held.tile([P, T], U32, name="tok_codes", align_bytes=64)
-        tok_scales = held.tile([P, T], U8, name="tok_scales", align_bytes=64)
-        hs_codes = held.tile([P, T], U32, name="hs_codes", align_bytes=64)
-        hs_scales = held.tile([P, T], U8, name="hs_scales", align_bytes=64)
 
-        sources = {("x", c): xT[:, c * CHUNK : (c + 1) * CHUNK] for c in range(T // CHUNK)}
-        for e in range(E + 1):
-            sources["w1", e] = w1[e]
-            sources["w2", e] = w2[e]
-        for h in range(2):
-            sources["w1", E, h] = w1[E][:, h * PAIR : (h + 1) * PAIR]
-            sources["x", 0, h] = xT[:, h * PAIR : (h + 1) * PAIR]
-        order = [("w1", E, 0), ("w1", E, 1), ("x", 0, 0), ("x", 0, 1), ("x", 1), ("x", 2)]
-        order.extend([("w1", 0), ("w1", 1)])
-        for q in range(PAIRS):
-            order.extend([("w1", 2 * q + 2), ("w1", 2 * q + 3)] if q + 1 < PAIRS else [("w2", E)])
-            order.extend([("w2", 2 * q), ("w2", 2 * q + 1)])
+        def mx_tiles(pool, name, width):
+            return (
+                pool.tile([P, width], U32, name=name + "_codes", align_bytes=64),
+                pool.tile([P, width], U8, name=name + "_scales", align_bytes=64),
+            )
+
+        slots = mx_tiles(held, "slot", S)
+        tokens = mx_tiles(held, "token", T)
+        hidden_s = mx_tiles(held, "hs", T)
+        ws1 = mx_tiles(held, "ws1", WIDTH)
+        ws2 = mx_tiles(held, "ws2", WIDTH)
+
+        def load(name, source, offset):
+            raw = rawp.tile([P, PACK, source.shape[1]], F32, name=name, offset=offset)
+            nc.sync.dma_start(out=raw[:], in_=source.rearrange("(p j) c -> p j c", j=PACK))
+            return raw
+
         raws = {}
+        order = [("w1", 0), ("w1", 1), ("w2", 0), ("w1", 2), ("w2", 1), ("w1", 3), ("w2", 2), ("w2", PAIRS), ("w2", 3)]
 
         def load_next():
             if len(raws) < len(order):
-                key = order[len(raws)]
-                raw = rawp.tile([P, PACK, sources[key].shape[1]], F32, name="raw")
-                nc.sync.dma_start(out=raw[:], in_=sources[key].rearrange("(p j) c -> p j c", j=PACK))
-                raws[key] = raw
-                if key == ("x", 1):
-                    nc.sync.dma_start(offsets[:], offs)
-                if key == ("w1", 3):
+                kind, q = order[len(raws)]
+                region = (len(raws) + 2) % REGIONS
+                if q == PAIRS:
+                    raws[kind, q] = load("shared_w2", w2[E], region * REGION)
+                else:
+                    raw = rawp.tile([P, 2, PACK, WIDTH], F32, name=f"raw{region}", offset=region * REGION)
+                    source = (w1 if kind == "w1" else w2)[2 * q : 2 * q + 2]
+                    nc.sync.dma_start(out=raw[:], in_=source.rearrange("e (p j) c -> p e j c", j=PACK))
+                    raws[kind, q] = raw
+                if (kind, q) == ("w1", 1):
                     nc.sync.dma_start(out=gate_sb[:], in_=gate[0:P, :])
 
-        def cast(key, grouped, on_vector):
-            raw = raws[key]
-            quads = raw.shape[2] // 4
-            first = key[2] * quads if len(key) == 3 else 0
-            if key[0] == "w1":
-                dst = grouped.rearrange("p (t m j) -> p m j t", t=PACK, j=PACK)
-            else:
-                dst = grouped.rearrange("p (m i j) -> p m j i", i=4, j=PACK)
-            dst = dst[:, first : first + quads]
-            src = raw[:].rearrange("p j (m i) -> p m j i", i=4)
+        def copy_shared(dst, src, on_vector):
             if on_vector > 0:
                 nc.vector.tensor_copy(out=dst[:, :on_vector], in_=src[:, :on_vector])
-            if on_vector < quads:
+            if on_vector < src.shape[1]:
                 nc.scalar.copy(out=dst[:, on_vector:], in_=src[:, on_vector:])
-            load_next()
 
-        def quantize(codes, scales, grouped):
-            nc.vector.quantize_mx(out=codes.bitcast(FP8X4), scales=scales, in_=grouped)
+        def by_quads(raw):
+            return raw.rearrange("p j (m i) -> p m j i", i=4)
+
+        def plain(grouped):
+            return grouped.rearrange("p (m i j) -> p m j i", i=4, j=PACK)
+
+        def permuted(grouped):
+            return grouped.rearrange("p (t m j) -> p m j t", t=PACK, j=PACK)
+
+        def quantize(dst, cols, grouped):
+            nc.vector.quantize_mx(out=dst[0][:, cols].bitcast(FP8X4), scales=dst[1][:, cols], in_=grouped)
 
         def mx(dst, w, wcols, x, xcols):
             nc.tensor.matmul_mx(
@@ -117,15 +121,6 @@ def tile_moe_shr_mlp_relu2_kernel(tc, xT, w1, w2, gate, offs, out):
                 mx(bank[:, t, :], w, slice(w0 + t * P, w0 + (t + 1) * P), x, slice(x0, x0 + C))
             nc.scalar.activation(relu_out.rearrange("p (c t) -> p c t", t=PACK), bank[:].rearrange("p t c -> p c t"), RELU)
 
-        slots = (slot_codes, slot_scales)
-        tokens = (tok_codes, tok_scales)
-        hidden_s = (hs_codes, hs_scales)
-        ws1 = (held.tile([P, WIDTH], U32, name="ws1c", align_bytes=64), held.tile([P, WIDTH], U8, name="ws1s", align_bytes=64))
-        ws2 = (held.tile([P, WIDTH], U32, name="ws2c", align_bytes=64), held.tile([P, WIDTH], U8, name="ws2s", align_bytes=64))
-
-        for n in range(8):
-            load_next()
-
         xb = {}
 
         def split_planes(c):
@@ -135,8 +130,7 @@ def tile_moe_shr_mlp_relu2_kernel(tc, xT, w1, w2, gate, offs, out):
             )
 
         def quantize_tokens(c, t0, t1):
-            cols = slice(c * CHUNK + t0, c * CHUNK + t1)
-            quantize(tok_codes[:, cols], tok_scales[:, cols], xb[c][:, PACK * t0 : PACK * t1])
+            quantize(tokens, slice(c * CHUNK + t0, c * CHUNK + t1), xb[c][:, PACK * t0 : PACK * t1])
 
         hsb = {}
 
@@ -150,41 +144,53 @@ def tile_moe_shr_mlp_relu2_kernel(tc, xT, w1, w2, gate, offs, out):
                 nc.scalar.activation(hsb[c][:, half], r, SQUARE)
 
         def shared_hidden(c):
-            cols = slice(c * CHUNK, (c + 1) * CHUNK)
-            quantize(hs_codes[:, cols], hs_scales[:, cols], hsb[c][:])
+            quantize(hidden_s, slice(c * CHUNK, (c + 1) * CHUNK), hsb[c][:])
 
         picked = {}
+        woven = {}
 
         def gather(h, room):
             picked[h] = room
             o = offsets[:, h * (HALF // 16) : (h + 1) * (HALF // 16)]
             for u in range(2):
-                nc.vector.tensor_copy(picked[h][:, u * HALF : (u + 1) * HALF], planes[:, u * T : (u + 1) * T].indirect(o))
+                nc.vector.tensor_copy(room[:, u * HALF : (u + 1) * HALF], planes[:, u * T : (u + 1) * T].indirect(o))
 
         def weave(h):
-            sb = three.tile([P, PACK * HALF], BF16, name="xb", align_bytes=64)
+            woven[h] = three.tile([P, PACK * HALF], BF16, name="xb", align_bytes=64)
             nc.vector.tensor_copy(
-                out=sb[:].bitcast(I32).rearrange("p (s u) -> p s u", u=2),
+                out=woven[h][:].bitcast(I32).rearrange("p (s u) -> p s u", u=2),
                 in_=picked[h].bitcast(I32).rearrange("p (u s) -> p s u", u=2),
             )
-            return sb
+
+        def quantize_slots(h):
+            quantize(slots, slice(h * HALF, (h + 1) * HALF), woven[h][:])
 
         grouped = {}
         codes = {}
         hb = {}
         hq = {}
         yg = {}
+        ONE = PACK * WIDTH
 
-        def cast_w(kind, q, u, on_vector):
-            if u == 0:
-                grouped[kind, q] = three.tile([P, 2 * PACK * WIDTH], BF16, name="wb", align_bytes=64)
-            cast((kind, 2 * q + u), grouped[kind, q][:, u * PACK * WIDTH : (u + 1) * PACK * WIDTH], on_vector)
+        def cast_w1(q, on_vector):
+            grouped["w1", q] = three.tile([P, 2 * ONE], BF16, name="wb", align_bytes=64)
+            for u in range(2):
+                copy_shared(permuted(grouped["w1", q][:, u * ONE : (u + 1) * ONE]), by_quads(raws["w1", q][:, u]), on_vector[u])
+            load_next()
+
+        def cast_w2(q):
+            grouped["w2", q] = three.tile([P, 2 * ONE], BF16, name="wb", align_bytes=64)
+            for a in range(2):
+                nc.vector.tensor_copy(
+                    out=grouped["w2", q][:, a * ONE : (a + 1) * ONE].rearrange("p (e m i j) -> p e m j i", e=2, i=4, j=PACK),
+                    in_=raws["w2", q][:, :, :, a * PAIR : (a + 1) * PAIR].rearrange("p e j (m i) -> p e m j i", i=4),
+                )
+            load_next()
 
         def quantize_w(kind, q):
-            wc = two.tile([P, 2 * WIDTH], U32, name=kind + "c", align_bytes=64)
-            ws = two.tile([P, 2 * WIDTH], U8, name=kind + "s", align_bytes=64)
-            codes[kind, q] = (wc, ws)
-            quantize(wc[:], ws[:], grouped[kind, q][:])
+            codes[kind, q] = mx_tiles(two, kind, 2 * WIDTH)
+            for a in range(2):
+                quantize(codes[kind, q], slice(a * WIDTH, (a + 1) * WIDTH), grouped[kind, q][:, a * ONE : (a + 1) * ONE])
 
         def routed_first(q):
             r = two.tile([P, PACK * PAIR], F32, name="r")
@@ -194,10 +200,8 @@ def tile_moe_shr_mlp_relu2_kernel(tc, xT, w1, w2, gate, offs, out):
             nc.scalar.activation(hb[q][:], r[:], SQUARE)
 
         def routed_hidden(q):
-            hc = held.tile([P, PAIR], U32, name="hc", align_bytes=64)
-            hs = held.tile([P, PAIR], U8, name="hs", align_bytes=64)
-            hq[q] = (hc, hs)
-            quantize(hc[:], hs[:], hb[q][:])
+            hq[q] = mx_tiles(held, "h", PAIR)
+            quantize(hq[q], slice(0, PAIR), hb[q][:])
 
         def routed_second(q):
             yg[q] = two.tile([P, BLOCKS, PAIR], F32, name="yg")
@@ -205,7 +209,7 @@ def tile_moe_shr_mlp_relu2_kernel(tc, xT, w1, w2, gate, offs, out):
                 bank = ps_y.tile([P, 2, PAIR], F32, name="bank_y")
                 for i in range(2):
                     for u in range(2):
-                        w0 = u * WIDTH + (2 * a + i) * P
+                        w0 = a * WIDTH + u * PAIR + i * P
                         mx(bank[:, i, u * C : (u + 1) * C], codes["w2", q], slice(w0, w0 + P), hq[q], slice(u * C, (u + 1) * C))
                 nc.vector.tensor_tensor(
                     out=yg[q][:, 2 * a : 2 * a + 2, :],
@@ -218,57 +222,60 @@ def tile_moe_shr_mlp_relu2_kernel(tc, xT, w1, w2, gate, offs, out):
             o = offsets[:, q * (PAIR // 16) : (q + 1) * (PAIR // 16)]
             nc.scalar.activation(z[b][:].indirect(o), yg[q][:, b, :], COPY)
 
-        wsb = three.tile([P, PACK * WIDTH], BF16, name="xb", align_bytes=64)
-        cast(("w1", E, 0), wsb[:], 0)
-        cast(("w1", E, 1), wsb[:], P // 2)
-        quantize(ws1[0][:], ws1[1][:], wsb[:])
-        xb[0] = three.tile([P, PACK * CHUNK], BF16, name="xb", align_bytes=64)
-        cast(("x", 0, 0), xb[0][:], EARLY_SPLIT)
+        quarter = REGION // 4
+        ws1_raw = [load(f"ws1_{h}", w1[E][:, h * PAIR : (h + 1) * PAIR], h * quarter) for h in range(2)]
+        x_first = [load(f"x0_{h}", xT[:, h * PAIR : (h + 1) * PAIR], (2 + h) * quarter) for h in range(2)]
+        x_raw = {1: load("x1", xT[:, CHUNK : 2 * CHUNK], REGION)}
+        nc.sync.dma_start(offsets[:], offs)
+        x_raw[2] = load("x2", xT[:, 2 * CHUNK :], REGION + 2 * quarter)
+        for n in range(REGIONS):
+            load_next()
+
+        wsb = three.tile([P, ONE], BF16, name="xb", align_bytes=64)
+        copy_shared(permuted(wsb[:])[:, : QUADS // 2], by_quads(ws1_raw[0][:]), 0)
+        copy_shared(permuted(wsb[:])[:, QUADS // 2 :], by_quads(ws1_raw[1][:]), QUADS // 2)
+        quantize(ws1, slice(0, WIDTH), wsb[:])
+        xb[0] = three.tile([P, ONE], BF16, name="xb", align_bytes=64)
+        copy_shared(plain(xb[0][:])[:, : QUADS // 2], by_quads(x_first[0][:]), EARLY_SPLIT)
         quantize_tokens(0, 0, PAIR)
-        cast(("x", 0, 1), xb[0][:], 0)
+        copy_shared(plain(xb[0][:])[:, QUADS // 2 :], by_quads(x_first[1][:]), 0)
         quantize_tokens(0, PAIR, CHUNK)
         shared_first(0)
         split_planes(0)
         for c in (1, 2):
-            xb[c] = three.tile([P, PACK * CHUNK], BF16, name="xb", align_bytes=64)
-            cast(("x", c), xb[c][:], P)
+            xb[c] = three.tile([P, ONE], BF16, name="xb", align_bytes=64)
+            copy_shared(plain(xb[c][:]), by_quads(x_raw[c][:]), QUADS)
             split_planes(c)
             quantize_tokens(c, 0, CHUNK)
-        cast_w("w1", 0, 0, 0)
-        gather(0, held.tile([P, 2 * HALF], U32, name="picked")[:])
-        sb = weave(0)
-        cast_w("w1", 0, 1, P)
-        quantize(slot_codes[:, :HALF], slot_scales[:, :HALF], sb[:])
-        quantize_w("w1", 0)
         shared_first(1)
+        for h in range(2):
+            gather(h, held.tile([P, 2 * HALF], U32, name="picked")[:])
+            weave(h)
+        quantize_slots(0)
+        cast_w1(0, (0, 0))
+        quantize_slots(1)
+        quantize_w("w1", 0)
+        shared_first(2, raws["w1", 0][:, 0].rearrange("p j c -> p (j c)"))
         routed_first(0)
 
         for q in range(PAIRS):
-            if q + 1 < PAIRS:
-                cast_w("w1", q + 1, 0, 0 if q == 0 else P)
-                cast_w("w1", q + 1, 1, P // 2 if q == 0 else P)
+            last = q + 1 == PAIRS
+            if last:
+                wsb = three.tile([P, ONE], BF16, name="xb", align_bytes=64)
+                copy_shared(plain(wsb[:]), by_quads(raws["w2", PAIRS][:]), QUADS)
             else:
-                wsb = three.tile([P, PACK * WIDTH], BF16, name="xb", align_bytes=64)
-                cast(("w2", E), wsb[:], P)
-            routed_hidden(q)
-            if q == 0:
-                shared_first(2, grouped["w1", 0][:].bitcast(F32))
-            if q + 1 < PAIRS:
+                cast_w1(q + 1, (QUADS // 2 if q == 0 else QUADS, QUADS))
                 quantize_w("w1", q + 1)
                 routed_first(q + 1)
+            routed_hidden(q)
+            cast_w2(q)
+            if last:
+                quantize(ws2, slice(0, WIDTH), wsb[:])
             else:
-                quantize(ws2[0][:], ws2[1][:], wsb[:])
-            cast_w("w2", q, 0, P)
-            cast_w("w2", q, 1, P)
-            if q < T // CHUNK:
                 shared_hidden(q)
             quantize_w("w2", q)
             routed_second(q)
-            if q == 0:
-                gather(1, grouped["w2", 0][:].bitcast(U32)[:, : 2 * HALF])
-                sb = weave(1)
-                quantize(slot_codes[:, HALF:], slot_scales[:, HALF:], sb[:])
-            if q + 1 < PAIRS:
+            if not last:
                 for b in range(BLOCKS):
                     scatter(q, b)
 

@@ -70,7 +70,7 @@ def tile_moe_shr_mlp_relu2_kernel(tc, xT, w1, w2, gate, offs, out):
             return raw
 
         raws = {}
-        order = [("w1", 0), ("w1", 1), ("w2", 0), ("w1", 2), ("w2", 1), ("w1", 3), ("w2", 2), ("w2", PAIRS), ("w2", 3)]
+        order = [("w1", 0), ("w1", 1), ("w1", 2), ("w2", 0), ("w1", 3), ("w2", 1), ("w2", PAIRS), ("w2", 2), ("w2", 3)]
 
         def load_next():
             if len(raws) < len(order):
@@ -83,7 +83,7 @@ def tile_moe_shr_mlp_relu2_kernel(tc, xT, w1, w2, gate, offs, out):
                     source = (w1 if kind == "w1" else w2)[2 * q : 2 * q + 2]
                     nc.sync.dma_start(out=raw[:], in_=source.rearrange("e (p j) c -> p e j c", j=PACK))
                     raws[kind, q] = raw
-                if (kind, q) == ("w1", 1):
+                if (kind, q) == ("w1", 2):
                     nc.sync.dma_start(out=gate_sb[:], in_=gate[0:P, :])
 
         def copy_shared(dst, src, on_vector):
@@ -257,25 +257,28 @@ def tile_moe_shr_mlp_relu2_kernel(tc, xT, w1, w2, gate, offs, out):
         quantize_w("w1", 0)
         shared_first(2, raws["w1", 0][:, 0].rearrange("p j c -> p (j c)"))
         routed_first(0)
+        cast_w1(1, (QUADS // 2, QUADS))
+        quantize_w("w1", 1)
+        routed_first(1)
+        for c in range(T // CHUNK):
+            shared_hidden(c)
 
         for q in range(PAIRS):
-            last = q + 1 == PAIRS
-            if last:
+            routed_hidden(q)
+            if q + 2 < PAIRS:
+                cast_w1(q + 2, (QUADS // 2 if q == 0 else QUADS, QUADS))
+                quantize_w("w1", q + 2)
+                routed_first(q + 2)
+            if q + 2 == PAIRS:
                 wsb = three.tile([P, ONE], BF16, name="xb", align_bytes=64)
                 copy_shared(plain(wsb[:]), by_quads(raws["w2", PAIRS][:]), QUADS)
-            else:
-                cast_w1(q + 1, (QUADS // 2 if q == 0 else QUADS, QUADS))
-                quantize_w("w1", q + 1)
-                routed_first(q + 1)
-            routed_hidden(q)
+                load_next()
             cast_w2(q)
-            if last:
+            if q + 2 == PAIRS:
                 quantize(ws2, slice(0, WIDTH), wsb[:])
-            else:
-                shared_hidden(q)
             quantize_w("w2", q)
             routed_second(q)
-            if not last:
+            if q + 1 < PAIRS:
                 for b in range(BLOCKS):
                     scatter(q, b)
 

@@ -38,6 +38,7 @@ def tile_moe_shr_mlp_relu2_kernel(tc, xT, w1, w2, gate, offs, out):
     with ExitStack() as ctx:
         held = ctx.enter_context(tc.tile_pool(name="held", bufs=1))
         rawp = ctx.enter_context(tc.tile_pool(name="rawp", bufs=1))
+        late = ctx.enter_context(tc.tile_pool(name="late", bufs=1))
         two = ctx.enter_context(tc.tile_pool(name="two", bufs=2))
         three = ctx.enter_context(tc.tile_pool(name="three", bufs=3))
         ps_a = ctx.enter_context(tc.psum_pool(name="ps_a", bufs=6))
@@ -60,7 +61,6 @@ def tile_moe_shr_mlp_relu2_kernel(tc, xT, w1, w2, gate, offs, out):
 
         slots = mx_tiles(held, "slot", S)
         tokens = mx_tiles(held, "token", T)
-        hidden_s = mx_tiles(held, "hs", T)
         ws1 = mx_tiles(held, "ws1", WIDTH)
         ws2 = mx_tiles(held, "ws2", WIDTH)
 
@@ -83,7 +83,7 @@ def tile_moe_shr_mlp_relu2_kernel(tc, xT, w1, w2, gate, offs, out):
                     source = (w1 if kind == "w1" else w2)[2 * q : 2 * q + 2]
                     nc.sync.dma_start(out=raw[:], in_=source.rearrange("e (p j) c -> p e j c", j=PACK))
                     raws[kind, q] = raw
-                if (kind, q) == ("w1", 2):
+                if (kind, q) == ("w2", 0):
                     nc.sync.dma_start(out=gate_sb[:], in_=gate[0:P, :])
 
         def copy_shared(dst, src, on_vector):
@@ -93,13 +93,13 @@ def tile_moe_shr_mlp_relu2_kernel(tc, xT, w1, w2, gate, offs, out):
                 nc.scalar.copy(out=dst[:, on_vector:], in_=src[:, on_vector:])
 
         def by_quads(raw):
-            return raw.rearrange("p j (m i) -> p m j i", i=4)
+            return raw.rearrange("p (g j) (m i) -> p m g i j", j=2, i=4)
 
         def plain(grouped):
-            return grouped.rearrange("p (m i j) -> p m j i", i=4, j=PACK)
+            return grouped.rearrange("p (m i g j) -> p m g i j", i=4, g=2, j=2)
 
         def permuted(grouped):
-            return grouped.rearrange("p (t m j) -> p m j t", t=PACK, j=PACK)
+            return grouped.rearrange("p (t m g j) -> p m g t j", t=PACK, g=2, j=2)
 
         def quantize(dst, cols, grouped):
             nc.vector.quantize_mx(out=dst[0][:, cols].bitcast(FP8X4), scales=dst[1][:, cols], in_=grouped)
@@ -143,8 +143,18 @@ def tile_moe_shr_mlp_relu2_kernel(tc, xT, w1, w2, gate, offs, out):
                     first_layer(ws1, 0, tokens, c * CHUNK + a * PAIR + u * C, r[:, u * PACK * C : (u + 1) * PACK * C])
                 nc.scalar.activation(hsb[c][:, half], r, SQUARE)
 
+        hidden_s = {}
+
         def shared_hidden(c):
-            quantize(hidden_s, slice(c * CHUNK, (c + 1) * CHUNK), hsb[c][:])
+            if c == 0:
+                hidden_s[c] = mx_tiles(held, "hs", CHUNK)
+            else:
+                start = (c - 1) * 5 * CHUNK
+                hidden_s[c] = (
+                    late.tile([P, CHUNK], U32, name=f"hs{c}_codes", align_bytes=64, offset=start),
+                    late.tile([P, CHUNK], U8, name=f"hs{c}_scales", align_bytes=64, offset=start + 4 * CHUNK),
+                )
+            quantize(hidden_s[c], slice(0, CHUNK), hsb[c][:])
 
         picked = {}
         woven = {}
@@ -173,18 +183,23 @@ def tile_moe_shr_mlp_relu2_kernel(tc, xT, w1, w2, gate, offs, out):
         ONE = PACK * WIDTH
 
         def cast_w1(q, on_vector):
-            grouped["w1", q] = three.tile([P, 2 * ONE], BF16, name="wb", align_bytes=64)
+            grouped["w1", q] = two.tile([P, 2 * ONE], BF16, name="wb", align_bytes=64)
             for u in range(2):
                 copy_shared(permuted(grouped["w1", q][:, u * ONE : (u + 1) * ONE]), by_quads(raws["w1", q][:, u]), on_vector[u])
             load_next()
 
         def cast_w2(q):
-            grouped["w2", q] = three.tile([P, 2 * ONE], BF16, name="wb", align_bytes=64)
+            if q == 2:
+                grouped["w2", q] = late.tile([P, 2 * ONE], BF16, name="wb_late", align_bytes=64, offset=0)
+            else:
+                grouped["w2", q] = two.tile([P, 2 * ONE], BF16, name="wb", align_bytes=64)
             for a in range(2):
-                nc.vector.tensor_copy(
-                    out=grouped["w2", q][:, a * ONE : (a + 1) * ONE].rearrange("p (e m i j) -> p e m j i", e=2, i=4, j=PACK),
-                    in_=raws["w2", q][:, :, :, a * PAIR : (a + 1) * PAIR].rearrange("p e j (m i) -> p e m j i", i=4),
-                )
+                for u in range(2):
+                    start = a * ONE + u * ONE // 2
+                    nc.vector.tensor_copy(
+                        out=plain(grouped["w2", q][:, start : start + ONE // 2]),
+                        in_=by_quads(raws["w2", q][:, u, :, a * PAIR : (a + 1) * PAIR]),
+                    )
             load_next()
 
         def quantize_w(kind, q):
@@ -223,7 +238,7 @@ def tile_moe_shr_mlp_relu2_kernel(tc, xT, w1, w2, gate, offs, out):
             nc.scalar.activation(z[b][:].indirect(o), yg[q][:, b, :], COPY)
 
         quarter = REGION // 4
-        ws1_raw = [load(f"ws1_{h}", w1[E][:, h * PAIR : (h + 1) * PAIR], h * quarter) for h in range(2)]
+        ws1_raw = load("ws1", w1[E], 0)
         x_first = [load(f"x0_{h}", xT[:, h * PAIR : (h + 1) * PAIR], (2 + h) * quarter) for h in range(2)]
         x_raw = {1: load("x1", xT[:, CHUNK : 2 * CHUNK], REGION)}
         nc.sync.dma_start(offsets[:], offs)
@@ -232,8 +247,7 @@ def tile_moe_shr_mlp_relu2_kernel(tc, xT, w1, w2, gate, offs, out):
             load_next()
 
         wsb = three.tile([P, ONE], BF16, name="xb", align_bytes=64)
-        copy_shared(permuted(wsb[:])[:, : QUADS // 2], by_quads(ws1_raw[0][:]), 0)
-        copy_shared(permuted(wsb[:])[:, QUADS // 2 :], by_quads(ws1_raw[1][:]), QUADS // 2)
+        copy_shared(permuted(wsb[:]), by_quads(ws1_raw[:]), 2 * EARLY_SPLIT)
         quantize(ws1, slice(0, WIDTH), wsb[:])
         xb[0] = three.tile([P, ONE], BF16, name="xb", align_bytes=64)
         copy_shared(plain(xb[0][:])[:, : QUADS // 2], by_quads(x_first[0][:]), EARLY_SPLIT)
@@ -257,16 +271,15 @@ def tile_moe_shr_mlp_relu2_kernel(tc, xT, w1, w2, gate, offs, out):
         quantize_w("w1", 0)
         shared_first(2, raws["w1", 0][:, 0].rearrange("p j c -> p (j c)"))
         routed_first(0)
-        cast_w1(1, (QUADS // 2, QUADS))
+        cast_w1(1, (QUADS, QUADS))
         quantize_w("w1", 1)
         routed_first(1)
-        for c in range(T // CHUNK):
-            shared_hidden(c)
+        shared_hidden(0)
 
         for q in range(PAIRS):
             routed_hidden(q)
             if q + 2 < PAIRS:
-                cast_w1(q + 2, (QUADS // 2 if q == 0 else QUADS, QUADS))
+                cast_w1(q + 2, (QUADS, QUADS))
                 quantize_w("w1", q + 2)
                 routed_first(q + 2)
             if q + 2 == PAIRS:
@@ -278,6 +291,9 @@ def tile_moe_shr_mlp_relu2_kernel(tc, xT, w1, w2, gate, offs, out):
                 quantize(ws2, slice(0, WIDTH), wsb[:])
             quantize_w("w2", q)
             routed_second(q)
+            if q == 2:
+                shared_hidden(1)
+                shared_hidden(2)
             if q + 1 < PAIRS:
                 for b in range(BLOCKS):
                     scatter(q, b)
@@ -287,6 +303,6 @@ def tile_moe_shr_mlp_relu2_kernel(tc, xT, w1, w2, gate, offs, out):
             for c in range(T // CHUNK):
                 cols = slice(c * CHUNK, (c + 1) * CHUNK)
                 bank = ps_a.tile([P, CHUNK], F32, name="bank_a")
-                mx(bank[:], ws2, slice(b * P, (b + 1) * P), hidden_s, cols)
+                mx(bank[:], ws2, slice(b * P, (b + 1) * P), hidden_s[c], slice(0, CHUNK))
                 nc.vector.tensor_tensor(out=z[b][:, cols], in0=bank[:], in1=z[b][:, cols], op=ADD)
                 nc.sync.dma_start(out=out[b * P : (b + 1) * P, cols], in_=z[b][:, cols])

@@ -46,9 +46,10 @@ def tile_moe_shr_mlp_relu2_kernel(tc, xT, w1, w2, gate, offs, out):
 
         offsets = held.tile([P, S // 16], U16, name="offsets")
         z = [held.tile([P, T], F32, name=f"z{b}") for b in range(BLOCKS)]
-        for b in range(BLOCKS - 1):
-            nc.vector.memset(z[b][:], 0.0)
-        nc.gpsimd.memset(z[BLOCKS - 1][:], 0.0)
+        nc.vector.memset(z[0][:], 0.0)
+        nc.vector.memset(z[1][:], 0.0)
+        nc.scalar.copy(out=z[2][:], in_=z[0][:])
+        nc.gpsimd.memset(z[3][:], 0.0)
 
         gate_sb = held.tile([P, S], F32, name="gate_sb")
         planes = held.tile([P, 2 * T], U32, name="planes")
@@ -123,10 +124,10 @@ def tile_moe_shr_mlp_relu2_kernel(tc, xT, w1, w2, gate, offs, out):
 
         xb = {}
 
-        def split_planes(c):
+        def split_planes(c, t0, t1):
             nc.vector.tensor_copy(
-                out=planes[:].bitcast(I32).rearrange("p (u t) -> p u t", u=2)[:, :, c * CHUNK : (c + 1) * CHUNK],
-                in_=xb[c][:].bitcast(I32).rearrange("p (t u) -> p u t", u=2),
+                out=planes[:].bitcast(I32).rearrange("p (u t) -> p u t", u=2)[:, :, c * CHUNK + t0 : c * CHUNK + t1],
+                in_=xb[c][:].bitcast(I32).rearrange("p (t u) -> p u t", u=2)[:, :, t0:t1],
             )
 
         def quantize_tokens(c, t0, t1):
@@ -156,25 +157,6 @@ def tile_moe_shr_mlp_relu2_kernel(tc, xT, w1, w2, gate, offs, out):
                 )
             quantize(hidden_s[c], slice(0, CHUNK), hsb[c][:])
 
-        picked = {}
-        woven = {}
-
-        def gather(h, room):
-            picked[h] = room
-            o = offsets[:, h * (HALF // 16) : (h + 1) * (HALF // 16)]
-            for u in range(2):
-                nc.vector.tensor_copy(room[:, u * HALF : (u + 1) * HALF], planes[:, u * T : (u + 1) * T].indirect(o))
-
-        def weave(h):
-            woven[h] = three.tile([P, PACK * HALF], BF16, name="xb", align_bytes=64)
-            nc.vector.tensor_copy(
-                out=woven[h][:].bitcast(I32).rearrange("p (s u) -> p s u", u=2),
-                in_=picked[h].bitcast(I32).rearrange("p (u s) -> p s u", u=2),
-            )
-
-        def quantize_slots(h):
-            quantize(slots, slice(h * HALF, (h + 1) * HALF), woven[h][:])
-
         grouped = {}
         codes = {}
         hb = {}
@@ -194,12 +176,10 @@ def tile_moe_shr_mlp_relu2_kernel(tc, xT, w1, w2, gate, offs, out):
             else:
                 grouped["w2", q] = two.tile([P, 2 * ONE], BF16, name="wb", align_bytes=64)
             for a in range(2):
-                for u in range(2):
-                    start = a * ONE + u * ONE // 2
-                    nc.vector.tensor_copy(
-                        out=plain(grouped["w2", q][:, start : start + ONE // 2]),
-                        in_=by_quads(raws["w2", q][:, u, :, a * PAIR : (a + 1) * PAIR]),
-                    )
+                nc.vector.tensor_copy(
+                    out=grouped["w2", q][:, a * ONE : (a + 1) * ONE].rearrange("p (e m i j) -> p e m j i", e=2, i=4, j=PACK),
+                    in_=raws["w2", q][:, :, :, a * PAIR : (a + 1) * PAIR].rearrange("p e j (m i) -> p e m j i", i=4),
+                )
             load_next()
 
         def quantize_w(kind, q):
@@ -255,26 +235,38 @@ def tile_moe_shr_mlp_relu2_kernel(tc, xT, w1, w2, gate, offs, out):
         copy_shared(plain(xb[0][:])[:, QUADS // 2 :], by_quads(x_first[1][:]), 0)
         quantize_tokens(0, PAIR, CHUNK)
         shared_first(0)
-        split_planes(0)
+        split_planes(0, 0, CHUNK)
         for c in (1, 2):
             xb[c] = three.tile([P, ONE], BF16, name="xb", align_bytes=64)
-            copy_shared(plain(xb[c][:]), by_quads(x_raw[c][:]), QUADS)
-            split_planes(c)
+            for h in range(2):
+                quads = slice(h * QUADS // 2, (h + 1) * QUADS // 2)
+                nc.vector.tensor_copy(out=plain(xb[c][:])[:, quads], in_=by_quads(x_raw[c][:])[:, quads])
+            for h in range(2):
+                split_planes(c, h * PAIR, (h + 1) * PAIR)
             quantize_tokens(c, 0, CHUNK)
         shared_first(1)
-        for h in range(2):
-            gather(h, held.tile([P, 2 * HALF], U32, name="picked")[:])
-            weave(h)
-        quantize_slots(0)
+        picked = late.tile([P, 2 * S], U32, name="picked", align_bytes=64, offset=0)
+        halves = [slice(h * HALF, (h + 1) * HALF) for h in range(2)]
+        nc.vector.tensor_copy(picked[:, :S], planes[:, :T].indirect(offsets[:]))
+        for half in halves:
+            o = offsets[:, half.start // 16 : half.stop // 16]
+            nc.vector.tensor_copy(picked[:, S + half.start : S + half.stop], planes[:, T:].indirect(o))
+        woven = held.tile([P, PACK * S], BF16, name="woven", align_bytes=64)
+        for half in halves:
+            nc.vector.tensor_copy(
+                out=woven[:].bitcast(I32).rearrange("p (s u) -> p s u", u=2)[:, half],
+                in_=picked[:].bitcast(I32).rearrange("p (u s) -> p s u", u=2)[:, half],
+            )
+        for half in halves:
+            quantize(slots, half, woven[:, PACK * half.start : PACK * half.stop])
+        shared_hidden(0)
         cast_w1(0, (0, 0))
-        quantize_slots(1)
         quantize_w("w1", 0)
         shared_first(2, raws["w1", 0][:, 0].rearrange("p j c -> p (j c)"))
         routed_first(0)
         cast_w1(1, (QUADS, QUADS))
         quantize_w("w1", 1)
         routed_first(1)
-        shared_hidden(0)
 
         for q in range(PAIRS):
             routed_hidden(q)
@@ -301,8 +293,8 @@ def tile_moe_shr_mlp_relu2_kernel(tc, xT, w1, w2, gate, offs, out):
         for b in range(BLOCKS):
             scatter(PAIRS - 1, b)
             for c in range(T // CHUNK):
-                cols = slice(c * CHUNK, (c + 1) * CHUNK)
                 bank = ps_a.tile([P, CHUNK], F32, name="bank_a")
                 mx(bank[:], ws2, slice(b * P, (b + 1) * P), hidden_s[c], slice(0, CHUNK))
+                cols = slice(c * CHUNK, (c + 1) * CHUNK)
                 nc.vector.tensor_tensor(out=z[b][:, cols], in0=bank[:], in1=z[b][:, cols], op=ADD)
                 nc.sync.dma_start(out=out[b * P : (b + 1) * P, cols], in_=z[b][:, cols])

@@ -71,7 +71,7 @@ def tile_moe_shr_mlp_relu2_kernel(tc, xT, w1, w2, gate, offs, out):
             return raw
 
         raws = {}
-        order = [("w1", 0), ("w1", 1), ("w1", 2), ("w2", 0), ("w1", 3), ("w2", 1), ("w2", PAIRS), ("w2", 2), ("w2", 3)]
+        order = [("w1", 0), ("w1", 1), ("w1", 2), ("w2", 0), ("w1", 3), ("w2", 1), ("w2", 2), ("w2", 3), ("w2", PAIRS)]
 
         def load_next():
             if len(raws) < len(order):
@@ -274,13 +274,7 @@ def tile_moe_shr_mlp_relu2_kernel(tc, xT, w1, w2, gate, offs, out):
                 cast_w1(q + 2, (QUADS, QUADS))
                 quantize_w("w1", q + 2)
                 routed_first(q + 2)
-            if q + 2 == PAIRS:
-                wsb = three.tile([P, ONE], BF16, name="xb", align_bytes=64)
-                copy_shared(plain(wsb[:]), by_quads(raws["w2", PAIRS][:]), QUADS)
-                load_next()
             cast_w2(q)
-            if q + 2 == PAIRS:
-                quantize(ws2, slice(0, WIDTH), wsb[:])
             quantize_w("w2", q)
             routed_second(q)
             if q == 2:
@@ -289,6 +283,13 @@ def tile_moe_shr_mlp_relu2_kernel(tc, xT, w1, w2, gate, offs, out):
             if q + 1 < PAIRS:
                 for b in range(BLOCKS):
                     scatter(q, b)
+
+        wsb = three.tile([P, ONE], BF16, name="xb", align_bytes=64)
+        for h in range(2):
+            quads = slice(h * QUADS // 2, (h + 1) * QUADS // 2)
+            nc.vector.tensor_copy(out=plain(wsb[:])[:, quads], in_=by_quads(raws["w2", PAIRS][:])[:, quads])
+        for h in range(2):
+            quantize(ws2, slice(h * PAIR, (h + 1) * PAIR), wsb[:, h * ONE // 2 : (h + 1) * ONE // 2])
 
         for b in range(BLOCKS):
             scatter(PAIRS - 1, b)

@@ -29,7 +29,7 @@ BLOCKS = N // P
 PAIRS = E // 2
 QUADS = WIDTH // 4
 REGION = 2 * PACK * WIDTH * 4
-REGIONS = 4
+REGIONS = 5
 EARLY_SPLIT = 40
 
 
@@ -39,6 +39,7 @@ def tile_moe_shr_mlp_relu2_kernel(tc, xT, w1, w2, gate, offs, out):
         held = ctx.enter_context(tc.tile_pool(name="held", bufs=1))
         rawp = ctx.enter_context(tc.tile_pool(name="rawp", bufs=1))
         late = ctx.enter_context(tc.tile_pool(name="late", bufs=1))
+        spare = ctx.enter_context(tc.tile_pool(name="spare", bufs=1))
         two = ctx.enter_context(tc.tile_pool(name="two", bufs=2))
         three = ctx.enter_context(tc.tile_pool(name="three", bufs=3))
         ps_a = ctx.enter_context(tc.psum_pool(name="ps_a", bufs=6))
@@ -71,7 +72,7 @@ def tile_moe_shr_mlp_relu2_kernel(tc, xT, w1, w2, gate, offs, out):
             return raw
 
         raws = {}
-        order = [("w1", 0), ("w1", 1), ("w1", 2), ("w2", 0), ("w1", 3), ("w2", 1), ("w2", 2), ("w2", 3), ("w2", PAIRS)]
+        order = [("w1", 0), ("w1", 1), ("w2", 0), ("w1", 2), ("w2", 1), ("w1", 3), ("w2", 2), ("w2", 3), ("w2", PAIRS)]
 
         def load_next():
             if len(raws) < len(order):
@@ -152,8 +153,8 @@ def tile_moe_shr_mlp_relu2_kernel(tc, xT, w1, w2, gate, offs, out):
             else:
                 start = (c - 1) * 5 * CHUNK
                 hidden_s[c] = (
-                    late.tile([P, CHUNK], U32, name=f"hs{c}_codes", align_bytes=64, offset=start),
-                    late.tile([P, CHUNK], U8, name=f"hs{c}_scales", align_bytes=64, offset=start + 4 * CHUNK),
+                    spare.tile([P, CHUNK], U32, name=f"hs{c}_codes", align_bytes=64, offset=start),
+                    spare.tile([P, CHUNK], U8, name=f"hs{c}_scales", align_bytes=64, offset=start + 4 * CHUNK),
                 )
             quantize(hidden_s[c], slice(0, CHUNK), hsb[c][:])
 
@@ -251,7 +252,7 @@ def tile_moe_shr_mlp_relu2_kernel(tc, xT, w1, w2, gate, offs, out):
         for half in halves:
             o = offsets[:, half.start // 16 : half.stop // 16]
             nc.vector.tensor_copy(picked[:, S + half.start : S + half.stop], planes[:, T:].indirect(o))
-        woven = held.tile([P, PACK * S], BF16, name="woven", align_bytes=64)
+        woven = spare.tile([P, PACK * S], BF16, name="woven", align_bytes=64, offset=0)
         for half in halves:
             nc.vector.tensor_copy(
                 out=woven[:].bitcast(I32).rearrange("p (s u) -> p s u", u=2)[:, half],
@@ -264,22 +265,18 @@ def tile_moe_shr_mlp_relu2_kernel(tc, xT, w1, w2, gate, offs, out):
         quantize_w("w1", 0)
         shared_first(2, raws["w1", 0][:, 0].rearrange("p j c -> p (j c)"))
         routed_first(0)
-        cast_w1(1, (QUADS, QUADS))
-        quantize_w("w1", 1)
-        routed_first(1)
 
         for q in range(PAIRS):
+            if q + 1 < PAIRS:
+                cast_w1(q + 1, (QUADS // 2 if q == 0 else QUADS, QUADS))
+                quantize_w("w1", q + 1)
+                routed_first(q + 1)
             routed_hidden(q)
-            if q + 2 < PAIRS:
-                cast_w1(q + 2, (QUADS, QUADS))
-                quantize_w("w1", q + 2)
-                routed_first(q + 2)
             cast_w2(q)
+            if q < 2:
+                shared_hidden(q + 1)
             quantize_w("w2", q)
             routed_second(q)
-            if q == 2:
-                shared_hidden(1)
-                shared_hidden(2)
             if q + 1 < PAIRS:
                 for b in range(BLOCKS):
                     scatter(q, b)

@@ -151,10 +151,10 @@ def tile_moe_shr_mlp_relu2_kernel(tc, xT, w1, w2, gate, offs, out):
             if c == 0:
                 hidden_s[c] = mx_tiles(held, "hs", CHUNK)
             else:
-                start = (c - 1) * 5 * CHUNK
+                pool = spare if c == 1 else late
                 hidden_s[c] = (
-                    spare.tile([P, CHUNK], U32, name=f"hs{c}_codes", align_bytes=64, offset=start),
-                    spare.tile([P, CHUNK], U8, name=f"hs{c}_scales", align_bytes=64, offset=start + 4 * CHUNK),
+                    pool.tile([P, CHUNK], U32, name=f"hs{c}_codes", align_bytes=64, offset=0),
+                    pool.tile([P, CHUNK], U8, name=f"hs{c}_scales", align_bytes=64, offset=4 * CHUNK),
                 )
             quantize(hidden_s[c], slice(0, CHUNK), hsb[c][:])
 
@@ -268,15 +268,17 @@ def tile_moe_shr_mlp_relu2_kernel(tc, xT, w1, w2, gate, offs, out):
 
         for q in range(PAIRS):
             if q + 1 < PAIRS:
-                cast_w1(q + 1, (QUADS // 2 if q == 0 else QUADS, QUADS))
+                cast_w1(q + 1, (QUADS, QUADS))
                 quantize_w("w1", q + 1)
                 routed_first(q + 1)
             routed_hidden(q)
             cast_w2(q)
-            if q < 2:
-                shared_hidden(q + 1)
+            if q == 0:
+                shared_hidden(1)
             quantize_w("w2", q)
             routed_second(q)
+            if q == 2:
+                shared_hidden(2)
             if q + 1 < PAIRS:
                 for b in range(BLOCKS):
                     scatter(q, b)

@@ -40,6 +40,7 @@ def tile_moe_shr_mlp_relu2_kernel(tc, xT, w1, w2, gate, offs, out):
         rawp = ctx.enter_context(tc.tile_pool(name="rawp", bufs=1))
         late = ctx.enter_context(tc.tile_pool(name="late", bufs=1))
         spare = ctx.enter_context(tc.tile_pool(name="spare", bufs=1))
+        xp = ctx.enter_context(tc.tile_pool(name="xp", bufs=1))
         two = ctx.enter_context(tc.tile_pool(name="two", bufs=2))
         three = ctx.enter_context(tc.tile_pool(name="three", bufs=3))
         ps_a = ctx.enter_context(tc.psum_pool(name="ps_a", bufs=6))
@@ -80,6 +81,8 @@ def tile_moe_shr_mlp_relu2_kernel(tc, xT, w1, w2, gate, offs, out):
                 region = (len(raws) + 2) % REGIONS
                 if q == PAIRS:
                     raws[kind, q] = load("shared_w2", w2[E], region * REGION)
+                elif (kind, q) == ("w2", 0):
+                    raws[kind, q] = load("w2_1", w2[1], region * REGION + REGION // 2)
                 else:
                     raw = rawp.tile([P, 2, PACK, WIDTH], F32, name=f"raw{region}", offset=region * REGION)
                     source = (w1 if kind == "w1" else w2)[2 * q : 2 * q + 2]
@@ -136,9 +139,10 @@ def tile_moe_shr_mlp_relu2_kernel(tc, xT, w1, w2, gate, offs, out):
 
         hsb = {}
 
-        def shared_first(c, room=None):
-            hsb[c] = three.tile([P, PACK * CHUNK], BF16, name="hsb", align_bytes=64)
-            for a in range(2):
+        def shared_first(c, parts=(0, 1), room=None):
+            if 0 in parts:
+                hsb[c] = three.tile([P, PACK * CHUNK], BF16, name="hsb", align_bytes=64)
+            for a in parts:
                 half = slice(a * PACK * PAIR, (a + 1) * PACK * PAIR)
                 r = two.tile([P, PACK * PAIR], F32, name="r")[:] if room is None else room[:, half]
                 for u in range(2):
@@ -165,6 +169,9 @@ def tile_moe_shr_mlp_relu2_kernel(tc, xT, w1, w2, gate, offs, out):
         yg = {}
         ONE = PACK * WIDTH
 
+        def rounded(slot):
+            return xp.tile([P, ONE], BF16, name=f"xb{slot}", align_bytes=64)
+
         def cast_w1(q, on_vector):
             grouped["w1", q] = two.tile([P, 2 * ONE], BF16, name="wb", align_bytes=64)
             for u in range(2):
@@ -177,6 +184,10 @@ def tile_moe_shr_mlp_relu2_kernel(tc, xT, w1, w2, gate, offs, out):
             else:
                 grouped["w2", q] = two.tile([P, 2 * ONE], BF16, name="wb", align_bytes=64)
             for a in range(2):
+                if q == 0:
+                    quads = slice(a * QUADS // 2, (a + 1) * QUADS // 2)
+                    nc.vector.tensor_copy(out=plain(grouped["w2", q][:, :ONE])[:, quads], in_=by_quads(raws["w2", q][:])[:, quads])
+                    continue
                 nc.vector.tensor_copy(
                     out=grouped["w2", q][:, a * ONE : (a + 1) * ONE].rearrange("p (e m i j) -> p e m j i", e=2, i=4, j=PACK),
                     in_=raws["w2", q][:, :, :, a * PAIR : (a + 1) * PAIR].rearrange("p e j (m i) -> p e m j i", i=4),
@@ -185,6 +196,11 @@ def tile_moe_shr_mlp_relu2_kernel(tc, xT, w1, w2, gate, offs, out):
 
         def quantize_w(kind, q):
             codes[kind, q] = mx_tiles(two, kind, 2 * WIDTH)
+            if (kind, q) == ("w2", 0):
+                quantize(codes[kind, q], slice(0, WIDTH), early[:])
+                for a in range(2):
+                    quantize(codes[kind, q], slice(WIDTH + a * PAIR, WIDTH + (a + 1) * PAIR), grouped[kind, q][:, a * ONE // 2 : (a + 1) * ONE // 2])
+                return
             for a in range(2):
                 quantize(codes[kind, q], slice(a * WIDTH, (a + 1) * WIDTH), grouped[kind, q][:, a * ONE : (a + 1) * ONE])
 
@@ -205,7 +221,7 @@ def tile_moe_shr_mlp_relu2_kernel(tc, xT, w1, w2, gate, offs, out):
                 bank = ps_y.tile([P, 2, PAIR], F32, name="bank_y")
                 for i in range(2):
                     for u in range(2):
-                        w0 = a * WIDTH + u * PAIR + i * P
+                        w0 = a * WIDTH + u * PAIR + i * P if q else u * WIDTH + a * PAIR + i * P
                         mx(bank[:, i, u * C : (u + 1) * C], codes["w2", q], slice(w0, w0 + P), hq[q], slice(u * C, (u + 1) * C))
                 nc.vector.tensor_tensor(
                     out=yg[q][:, 2 * a : 2 * a + 2, :],
@@ -224,13 +240,14 @@ def tile_moe_shr_mlp_relu2_kernel(tc, xT, w1, w2, gate, offs, out):
         x_raw = {1: load("x1", xT[:, CHUNK : 2 * CHUNK], REGION)}
         nc.sync.dma_start(offsets[:], offs)
         x_raw[2] = load("x2", xT[:, 2 * CHUNK :], REGION + 2 * quarter)
+        early_raw = load("w2_0", w2[0], 4 * REGION)
         for n in range(REGIONS):
             load_next()
 
-        wsb = three.tile([P, ONE], BF16, name="xb", align_bytes=64)
+        wsb = rounded(0)
         copy_shared(permuted(wsb[:]), by_quads(ws1_raw[:]), 2 * EARLY_SPLIT)
         quantize(ws1, slice(0, WIDTH), wsb[:])
-        xb[0] = three.tile([P, ONE], BF16, name="xb", align_bytes=64)
+        xb[0] = rounded(1)
         copy_shared(plain(xb[0][:])[:, : QUADS // 2], by_quads(x_first[0][:]), EARLY_SPLIT)
         quantize_tokens(0, 0, PAIR)
         copy_shared(plain(xb[0][:])[:, QUADS // 2 :], by_quads(x_first[1][:]), 0)
@@ -238,7 +255,7 @@ def tile_moe_shr_mlp_relu2_kernel(tc, xT, w1, w2, gate, offs, out):
         shared_first(0)
         split_planes(0, 0, CHUNK)
         for c in (1, 2):
-            xb[c] = three.tile([P, ONE], BF16, name="xb", align_bytes=64)
+            xb[c] = rounded((c + 1) % 3)
             for h in range(2):
                 quads = slice(h * QUADS // 2, (h + 1) * QUADS // 2)
                 nc.vector.tensor_copy(out=plain(xb[c][:])[:, quads], in_=by_quads(x_raw[c][:])[:, quads])
@@ -246,6 +263,16 @@ def tile_moe_shr_mlp_relu2_kernel(tc, xT, w1, w2, gate, offs, out):
                 split_planes(c, h * PAIR, (h + 1) * PAIR)
             quantize_tokens(c, 0, CHUNK)
         shared_first(1)
+        early = rounded(0)
+        nc.gpsimd.tensor_scalar(
+            out=early[:].rearrange("p (c j) -> p c j", j=PACK),
+            in0=early_raw[:].rearrange("p j c -> p c j"),
+            scalar1=1.0,
+            scalar2=0.0,
+            op0=MULT,
+            op1=ADD,
+        )
+        shared_first(2, (0,))
         picked = late.tile([P, 2 * S], U32, name="picked", align_bytes=64, offset=0)
         halves = [slice(h * HALF, (h + 1) * HALF) for h in range(2)]
         nc.vector.tensor_copy(picked[:, :S], planes[:, :T].indirect(offsets[:]))
@@ -263,7 +290,7 @@ def tile_moe_shr_mlp_relu2_kernel(tc, xT, w1, w2, gate, offs, out):
         shared_hidden(0)
         cast_w1(0, (0, 0))
         quantize_w("w1", 0)
-        shared_first(2, raws["w1", 0][:, 0].rearrange("p j c -> p (j c)"))
+        shared_first(2, (1,), raws["w1", 0][:, 1].rearrange("p j c -> p (j c)"))
         routed_first(0)
 
         for q in range(PAIRS):
@@ -283,7 +310,7 @@ def tile_moe_shr_mlp_relu2_kernel(tc, xT, w1, w2, gate, offs, out):
                 for b in range(BLOCKS):
                     scatter(q, b)
 
-        wsb = three.tile([P, ONE], BF16, name="xb", align_bytes=64)
+        wsb = rounded(1)
         for h in range(2):
             quads = slice(h * QUADS // 2, (h + 1) * QUADS // 2)
             nc.vector.tensor_copy(out=plain(wsb[:])[:, quads], in_=by_quads(raws["w2", PAIRS][:])[:, quads])

@@ -31,6 +31,7 @@ QUADS = WIDTH // 4
 REGION = 2 * PACK * WIDTH * 4
 REGIONS = 5
 EARLY_SPLIT = 40
+EARLY_COLUMNS = 256
 
 
 def tile_moe_shr_mlp_relu2_kernel(tc, xT, w1, w2, gate, offs, out):
@@ -82,7 +83,7 @@ def tile_moe_shr_mlp_relu2_kernel(tc, xT, w1, w2, gate, offs, out):
                 if q == PAIRS:
                     raws[kind, q] = load("shared_w2", w2[E], region * REGION)
                 elif (kind, q) == ("w2", 0):
-                    raws[kind, q] = load("w2_1", w2[1], region * REGION + REGION // 2)
+                    raws[kind, q] = load("w2_1b", w2[1][:, PAIR:], region * REGION + 3 * REGION // 4)
                 else:
                     raw = rawp.tile([P, 2, PACK, WIDTH], F32, name=f"raw{region}", offset=region * REGION)
                     source = (w1 if kind == "w1" else w2)[2 * q : 2 * q + 2]
@@ -152,14 +153,11 @@ def tile_moe_shr_mlp_relu2_kernel(tc, xT, w1, w2, gate, offs, out):
         hidden_s = {}
 
         def shared_hidden(c):
-            if c == 0:
-                hidden_s[c] = mx_tiles(held, "hs", CHUNK)
-            else:
-                pool = spare if c == 1 else late
-                hidden_s[c] = (
-                    pool.tile([P, CHUNK], U32, name=f"hs{c}_codes", align_bytes=64, offset=0),
-                    pool.tile([P, CHUNK], U8, name=f"hs{c}_scales", align_bytes=64, offset=4 * CHUNK),
-                )
+            at = {0: 1, 1: 3, 2: 4}[c] * REGION
+            hidden_s[c] = (
+                rawp.tile([P, CHUNK], U32, name=f"hs{c}_codes", align_bytes=64, offset=at),
+                rawp.tile([P, CHUNK], U8, name=f"hs{c}_scales", align_bytes=64, offset=at + 4 * CHUNK),
+            )
             quantize(hidden_s[c], slice(0, CHUNK), hsb[c][:])
 
         grouped = {}
@@ -173,21 +171,24 @@ def tile_moe_shr_mlp_relu2_kernel(tc, xT, w1, w2, gate, offs, out):
             return xp.tile([P, ONE], BF16, name=f"xb{slot}", align_bytes=64)
 
         def cast_w1(q, on_vector):
-            grouped["w1", q] = two.tile([P, 2 * ONE], BF16, name="wb", align_bytes=64)
+            if q == 1:
+                grouped["w1", q] = late.tile([P, 2 * ONE], BF16, name="wb_second", align_bytes=64, offset=0)
+            else:
+                grouped["w1", q] = two.tile([P, 2 * ONE], BF16, name="wb", align_bytes=64)
             for u in range(2):
                 copy_shared(permuted(grouped["w1", q][:, u * ONE : (u + 1) * ONE]), by_quads(raws["w1", q][:, u]), on_vector[u])
             load_next()
 
         def cast_w2(q):
+            if q == 0:
+                nc.vector.tensor_copy(out=plain(second[:, ONE // 2 :]), in_=by_quads(raws["w2", q][:]))
+                load_next()
+                return
             if q == 2:
                 grouped["w2", q] = late.tile([P, 2 * ONE], BF16, name="wb_late", align_bytes=64, offset=0)
             else:
                 grouped["w2", q] = two.tile([P, 2 * ONE], BF16, name="wb", align_bytes=64)
             for a in range(2):
-                if q == 0:
-                    quads = slice(a * QUADS // 2, (a + 1) * QUADS // 2)
-                    nc.vector.tensor_copy(out=plain(grouped["w2", q][:, :ONE])[:, quads], in_=by_quads(raws["w2", q][:])[:, quads])
-                    continue
                 nc.vector.tensor_copy(
                     out=grouped["w2", q][:, a * ONE : (a + 1) * ONE].rearrange("p (e m i j) -> p e m j i", e=2, i=4, j=PACK),
                     in_=raws["w2", q][:, :, :, a * PAIR : (a + 1) * PAIR].rearrange("p e j (m i) -> p e m j i", i=4),
@@ -195,11 +196,17 @@ def tile_moe_shr_mlp_relu2_kernel(tc, xT, w1, w2, gate, offs, out):
             load_next()
 
         def quantize_w(kind, q):
-            codes[kind, q] = mx_tiles(two, kind, 2 * WIDTH)
-            if (kind, q) == ("w2", 0):
+            if (kind, q) != ("w2", 0):
+                codes[kind, q] = mx_tiles(two, kind, 2 * WIDTH)
+            else:
+                codes[kind, q] = (
+                    late.tile([P, 2 * WIDTH], U32, name="first_codes", align_bytes=64, offset=0),
+                    late.tile([P, 2 * WIDTH], U8, name="first_scales", align_bytes=64, offset=8 * WIDTH),
+                )
                 quantize(codes[kind, q], slice(0, WIDTH), early[:])
+                routed_hidden(q)
                 for a in range(2):
-                    quantize(codes[kind, q], slice(WIDTH + a * PAIR, WIDTH + (a + 1) * PAIR), grouped[kind, q][:, a * ONE // 2 : (a + 1) * ONE // 2])
+                    quantize(codes[kind, q], slice(WIDTH + a * PAIR, WIDTH + (a + 1) * PAIR), second[:, a * ONE // 2 : (a + 1) * ONE // 2])
                 return
             for a in range(2):
                 quantize(codes[kind, q], slice(a * WIDTH, (a + 1) * WIDTH), grouped[kind, q][:, a * ONE : (a + 1) * ONE])
@@ -241,6 +248,7 @@ def tile_moe_shr_mlp_relu2_kernel(tc, xT, w1, w2, gate, offs, out):
         nc.sync.dma_start(offsets[:], offs)
         x_raw[2] = load("x2", xT[:, 2 * CHUNK :], REGION + 2 * quarter)
         early_raw = load("w2_0", w2[0], 4 * REGION)
+        second_raw = load("w2_1a", w2[1][:, :PAIR], 4 * REGION + REGION // 2)
         for n in range(REGIONS):
             load_next()
 
@@ -272,6 +280,15 @@ def tile_moe_shr_mlp_relu2_kernel(tc, xT, w1, w2, gate, offs, out):
             op0=MULT,
             op1=ADD,
         )
+        second = rounded(1)
+        nc.gpsimd.tensor_scalar(
+            out=second[:, : PACK * EARLY_COLUMNS].rearrange("p (c j) -> p c j", j=PACK),
+            in0=second_raw[:, :, :EARLY_COLUMNS].rearrange("p j c -> p c j"),
+            scalar1=1.0,
+            scalar2=0.0,
+            op0=MULT,
+            op1=ADD,
+        )
         shared_first(2, (0,))
         picked = late.tile([P, 2 * S], U32, name="picked", align_bytes=64, offset=0)
         halves = [slice(h * HALF, (h + 1) * HALF) for h in range(2)]
@@ -287,10 +304,9 @@ def tile_moe_shr_mlp_relu2_kernel(tc, xT, w1, w2, gate, offs, out):
             )
         for half in halves:
             quantize(slots, half, woven[:, PACK * half.start : PACK * half.stop])
-        shared_hidden(0)
-        cast_w1(0, (0, 0))
+        cast_w1(0, (0, 3 * QUADS // 4))
         quantize_w("w1", 0)
-        shared_first(2, (1,), raws["w1", 0][:, 1].rearrange("p j c -> p (j c)"))
+        shared_first(2, (1,), raws["w1", 0][:, 0].rearrange("p j c -> p (j c)"))
         routed_first(0)
 
         for q in range(PAIRS):
@@ -298,14 +314,13 @@ def tile_moe_shr_mlp_relu2_kernel(tc, xT, w1, w2, gate, offs, out):
                 cast_w1(q + 1, (QUADS, QUADS))
                 quantize_w("w1", q + 1)
                 routed_first(q + 1)
-            routed_hidden(q)
+            if q > 0:
+                routed_hidden(q)
             cast_w2(q)
-            if q == 0:
-                shared_hidden(1)
             quantize_w("w2", q)
+            if q > 0:
+                shared_hidden(q - 1)
             routed_second(q)
-            if q == 2:
-                shared_hidden(2)
             if q + 1 < PAIRS:
                 for b in range(BLOCKS):
                     scatter(q, b)

@@ -31,7 +31,6 @@ QUADS = WIDTH // 4
 REGION = 2 * PACK * WIDTH * 4
 REGIONS = 5
 EARLY_SPLIT = 40
-EARLY_COLUMNS = 256
 
 
 def tile_moe_shr_mlp_relu2_kernel(tc, xT, w1, w2, gate, offs, out):
@@ -83,7 +82,7 @@ def tile_moe_shr_mlp_relu2_kernel(tc, xT, w1, w2, gate, offs, out):
                 if q == PAIRS:
                     raws[kind, q] = load("shared_w2", w2[E], region * REGION)
                 elif (kind, q) == ("w2", 0):
-                    raws[kind, q] = load("w2_1b", w2[1][:, PAIR:], region * REGION + 3 * REGION // 4)
+                    raws[kind, q] = load("w2_1", w2[1], region * REGION + REGION // 2)
                 else:
                     raw = rawp.tile([P, 2, PACK, WIDTH], F32, name=f"raw{region}", offset=region * REGION)
                     source = (w1 if kind == "w1" else w2)[2 * q : 2 * q + 2]
@@ -165,6 +164,7 @@ def tile_moe_shr_mlp_relu2_kernel(tc, xT, w1, w2, gate, offs, out):
         hb = {}
         hq = {}
         yg = {}
+        relus = {}
         ONE = PACK * WIDTH
 
         def rounded(slot):
@@ -181,13 +181,10 @@ def tile_moe_shr_mlp_relu2_kernel(tc, xT, w1, w2, gate, offs, out):
 
         def cast_w2(q):
             if q == 0:
-                nc.vector.tensor_copy(out=plain(second[:, ONE // 2 :]), in_=by_quads(raws["w2", q][:]))
+                nc.vector.tensor_copy(out=plain(second[:]), in_=by_quads(raws["w2", q][:]))
                 load_next()
                 return
-            if q == 2:
-                grouped["w2", q] = late.tile([P, 2 * ONE], BF16, name="wb_late", align_bytes=64, offset=0)
-            else:
-                grouped["w2", q] = two.tile([P, 2 * ONE], BF16, name="wb", align_bytes=64)
+            grouped["w2", q] = two.tile([P, 2 * ONE], BF16, name="wb", align_bytes=64)
             for a in range(2):
                 nc.vector.tensor_copy(
                     out=grouped["w2", q][:, a * ONE : (a + 1) * ONE].rearrange("p (e m i j) -> p e m j i", e=2, i=4, j=PACK),
@@ -196,13 +193,14 @@ def tile_moe_shr_mlp_relu2_kernel(tc, xT, w1, w2, gate, offs, out):
             load_next()
 
         def quantize_w(kind, q):
-            if (kind, q) != ("w2", 0):
-                codes[kind, q] = mx_tiles(two, kind, 2 * WIDTH)
-            else:
+            if kind == "w2" and q in (0, 2):
                 codes[kind, q] = (
-                    late.tile([P, 2 * WIDTH], U32, name="first_codes", align_bytes=64, offset=0),
-                    late.tile([P, 2 * WIDTH], U8, name="first_scales", align_bytes=64, offset=8 * WIDTH),
+                    late.tile([P, 2 * WIDTH], U32, name=f"late_codes{q}", align_bytes=64, offset=0),
+                    late.tile([P, 2 * WIDTH], U8, name=f"late_scales{q}", align_bytes=64, offset=8 * WIDTH),
                 )
+            else:
+                codes[kind, q] = mx_tiles(two, kind, 2 * WIDTH)
+            if (kind, q) == ("w2", 0):
                 quantize(codes[kind, q], slice(0, WIDTH), early[:])
                 routed_hidden(q)
                 for a in range(2):
@@ -216,11 +214,17 @@ def tile_moe_shr_mlp_relu2_kernel(tc, xT, w1, w2, gate, offs, out):
             for u in range(2):
                 first_layer(codes["w1", q], u * WIDTH, slots, q * PAIR + u * C, r[:, u * PACK * C : (u + 1) * PACK * C])
             hb[q] = two.tile([P, PACK * PAIR], BF16, name="hb", align_bytes=64)
-            nc.scalar.activation(hb[q][:], r[:], SQUARE)
+            on_scalar = PACK * PAIR if q + 1 < PAIRS else PACK * C
+            nc.scalar.activation(hb[q][:, :on_scalar], r[:, :on_scalar], SQUARE)
+            relus[q] = r
 
         def routed_hidden(q):
             hq[q] = mx_tiles(held, "h", PAIR)
-            quantize(hq[q], slice(0, PAIR), hb[q][:])
+            if q + 1 < PAIRS:
+                quantize(hq[q], slice(0, PAIR), hb[q][:])
+            else:
+                quantize(hq[q], slice(0, C), hb[q][:, : PACK * C])
+                quantize(hq[q], slice(C, PAIR), last[:])
 
         def routed_second(q):
             yg[q] = two.tile([P, BLOCKS, PAIR], F32, name="yg")
@@ -248,7 +252,6 @@ def tile_moe_shr_mlp_relu2_kernel(tc, xT, w1, w2, gate, offs, out):
         nc.sync.dma_start(offsets[:], offs)
         x_raw[2] = load("x2", xT[:, 2 * CHUNK :], REGION + 2 * quarter)
         early_raw = load("w2_0", w2[0], 4 * REGION)
-        second_raw = load("w2_1a", w2[1][:, :PAIR], 4 * REGION + REGION // 2)
         for n in range(REGIONS):
             load_next()
 
@@ -281,14 +284,6 @@ def tile_moe_shr_mlp_relu2_kernel(tc, xT, w1, w2, gate, offs, out):
             op1=ADD,
         )
         second = rounded(1)
-        nc.gpsimd.tensor_scalar(
-            out=second[:, : PACK * EARLY_COLUMNS].rearrange("p (c j) -> p c j", j=PACK),
-            in0=second_raw[:, :, :EARLY_COLUMNS].rearrange("p j c -> p c j"),
-            scalar1=1.0,
-            scalar2=0.0,
-            op0=MULT,
-            op1=ADD,
-        )
         shared_first(2, (0,))
         picked = late.tile([P, 2 * S], U32, name="picked", align_bytes=64, offset=0)
         halves = [slice(h * HALF, (h + 1) * HALF) for h in range(2)]
@@ -314,9 +309,15 @@ def tile_moe_shr_mlp_relu2_kernel(tc, xT, w1, w2, gate, offs, out):
                 cast_w1(q + 1, (QUADS, QUADS))
                 quantize_w("w1", q + 1)
                 routed_first(q + 1)
-            if q > 0:
+            if q + 1 == PAIRS:
+                last = late.tile([P, PACK * C], BF16, name="hb_last", align_bytes=64, offset=0)
+                nc.vector.tensor_tensor(out=last[:], in0=relus[q][:, PACK * C :], in1=relus[q][:, PACK * C :], op=MULT)
+                cast_w2(q)
                 routed_hidden(q)
-            cast_w2(q)
+            else:
+                if q > 0:
+                    routed_hidden(q)
+                cast_w2(q)
             quantize_w("w2", q)
             if q > 0:
                 shared_hidden(q - 1)

@@ -85,8 +85,12 @@ def tile_moe_shr_mlp_relu2_kernel(tc, xT, w1, w2, gate, offs, out):
                     raws[kind, q] = load("w2_1", w2[1], region * REGION + REGION // 2)
                 else:
                     raw = rawp.tile([P, 2, PACK, WIDTH], F32, name=f"raw{region}", offset=region * REGION)
-                    source = (w1 if kind == "w1" else w2)[2 * q : 2 * q + 2]
-                    nc.sync.dma_start(out=raw[:], in_=source.rearrange("e (p j) c -> p e j c", j=PACK))
+                    source = (w1 if kind == "w1" else w2)[2 * q : 2 * q + 2].rearrange("e (p j) c -> p e j c", j=PACK)
+                    if (kind, q) == ("w1", 0):
+                        for u in range(2):
+                            nc.sync.dma_start(out=raw[:, u], in_=source[:, u])
+                    else:
+                        nc.sync.dma_start(out=raw[:], in_=source)
                     raws[kind, q] = raw
                 if (kind, q) == ("w2", 0):
                     nc.sync.dma_start(out=gate_sb[:], in_=gate[0:P, :])
@@ -164,7 +168,6 @@ def tile_moe_shr_mlp_relu2_kernel(tc, xT, w1, w2, gate, offs, out):
         hb = {}
         hq = {}
         yg = {}
-        relus = {}
         ONE = PACK * WIDTH
 
         def rounded(slot):
@@ -184,7 +187,10 @@ def tile_moe_shr_mlp_relu2_kernel(tc, xT, w1, w2, gate, offs, out):
                 nc.vector.tensor_copy(out=plain(second[:]), in_=by_quads(raws["w2", q][:]))
                 load_next()
                 return
-            grouped["w2", q] = two.tile([P, 2 * ONE], BF16, name="wb", align_bytes=64)
+            if q == 2:
+                grouped["w2", q] = late.tile([P, 2 * ONE], BF16, name="wb_late", align_bytes=64, offset=0)
+            else:
+                grouped["w2", q] = two.tile([P, 2 * ONE], BF16, name="wb", align_bytes=64)
             for a in range(2):
                 nc.vector.tensor_copy(
                     out=grouped["w2", q][:, a * ONE : (a + 1) * ONE].rearrange("p (e m i j) -> p e m j i", e=2, i=4, j=PACK),
@@ -193,14 +199,13 @@ def tile_moe_shr_mlp_relu2_kernel(tc, xT, w1, w2, gate, offs, out):
             load_next()
 
         def quantize_w(kind, q):
-            if kind == "w2" and q in (0, 2):
-                codes[kind, q] = (
-                    late.tile([P, 2 * WIDTH], U32, name=f"late_codes{q}", align_bytes=64, offset=0),
-                    late.tile([P, 2 * WIDTH], U8, name=f"late_scales{q}", align_bytes=64, offset=8 * WIDTH),
-                )
-            else:
+            if (kind, q) != ("w2", 0):
                 codes[kind, q] = mx_tiles(two, kind, 2 * WIDTH)
-            if (kind, q) == ("w2", 0):
+            else:
+                codes[kind, q] = (
+                    late.tile([P, 2 * WIDTH], U32, name="first_codes", align_bytes=64, offset=0),
+                    late.tile([P, 2 * WIDTH], U8, name="first_scales", align_bytes=64, offset=8 * WIDTH),
+                )
                 quantize(codes[kind, q], slice(0, WIDTH), early[:])
                 routed_hidden(q)
                 for a in range(2):
@@ -214,17 +219,11 @@ def tile_moe_shr_mlp_relu2_kernel(tc, xT, w1, w2, gate, offs, out):
             for u in range(2):
                 first_layer(codes["w1", q], u * WIDTH, slots, q * PAIR + u * C, r[:, u * PACK * C : (u + 1) * PACK * C])
             hb[q] = two.tile([P, PACK * PAIR], BF16, name="hb", align_bytes=64)
-            on_scalar = PACK * PAIR if q + 1 < PAIRS else PACK * C
-            nc.scalar.activation(hb[q][:, :on_scalar], r[:, :on_scalar], SQUARE)
-            relus[q] = r
+            nc.scalar.activation(hb[q][:], r[:], SQUARE)
 
         def routed_hidden(q):
             hq[q] = mx_tiles(held, "h", PAIR)
-            if q + 1 < PAIRS:
-                quantize(hq[q], slice(0, PAIR), hb[q][:])
-            else:
-                quantize(hq[q], slice(0, C), hb[q][:, : PACK * C])
-                quantize(hq[q], slice(C, PAIR), last[:])
+            quantize(hq[q], slice(0, PAIR), hb[q][:])
 
         def routed_second(q):
             yg[q] = two.tile([P, BLOCKS, PAIR], F32, name="yg")
@@ -261,7 +260,7 @@ def tile_moe_shr_mlp_relu2_kernel(tc, xT, w1, w2, gate, offs, out):
         xb[0] = rounded(1)
         copy_shared(plain(xb[0][:])[:, : QUADS // 2], by_quads(x_first[0][:]), EARLY_SPLIT)
         quantize_tokens(0, 0, PAIR)
-        copy_shared(plain(xb[0][:])[:, QUADS // 2 :], by_quads(x_first[1][:]), 0)
+        copy_shared(plain(xb[0][:])[:, QUADS // 2 :], by_quads(x_first[1][:]), EARLY_SPLIT)
         quantize_tokens(0, PAIR, CHUNK)
         shared_first(0)
         split_planes(0, 0, CHUNK)
@@ -284,7 +283,6 @@ def tile_moe_shr_mlp_relu2_kernel(tc, xT, w1, w2, gate, offs, out):
             op1=ADD,
         )
         second = rounded(1)
-        shared_first(2, (0,))
         picked = late.tile([P, 2 * S], U32, name="picked", align_bytes=64, offset=0)
         halves = [slice(h * HALF, (h + 1) * HALF) for h in range(2)]
         nc.vector.tensor_copy(picked[:, :S], planes[:, :T].indirect(offsets[:]))
@@ -299,9 +297,9 @@ def tile_moe_shr_mlp_relu2_kernel(tc, xT, w1, w2, gate, offs, out):
             )
         for half in halves:
             quantize(slots, half, woven[:, PACK * half.start : PACK * half.stop])
-        cast_w1(0, (0, 3 * QUADS // 4))
+        cast_w1(0, (0, QUADS // 2))
         quantize_w("w1", 0)
-        shared_first(2, (1,), raws["w1", 0][:, 0].rearrange("p j c -> p (j c)"))
+        shared_first(2, (0, 1), raws["w1", 0][:, 0].rearrange("p j c -> p (j c)"))
         routed_first(0)
 
         for q in range(PAIRS):
@@ -309,15 +307,9 @@ def tile_moe_shr_mlp_relu2_kernel(tc, xT, w1, w2, gate, offs, out):
                 cast_w1(q + 1, (QUADS, QUADS))
                 quantize_w("w1", q + 1)
                 routed_first(q + 1)
-            if q + 1 == PAIRS:
-                last = late.tile([P, PACK * C], BF16, name="hb_last", align_bytes=64, offset=0)
-                nc.vector.tensor_tensor(out=last[:], in0=relus[q][:, PACK * C :], in1=relus[q][:, PACK * C :], op=MULT)
-                cast_w2(q)
+            if q > 0:
                 routed_hidden(q)
-            else:
-                if q > 0:
-                    routed_hidden(q)
-                cast_w2(q)
+            cast_w2(q)
             quantize_w("w2", q)
             if q > 0:
                 shared_hidden(q - 1)

from contextlib import ExitStack

import concourse.mybir as mybir

K, T, E, C, H, N = 512, 1536, 8, 128, 512, 512
S = E * C
FLOPS = 2 * (S + T) * (K * H + H * N)
BYTES = 4 * (K * T + (E + 1) * (K * H + H * N) + S + N * T) + 2 * 128 * (S // 16)

F32 = mybir.dt.float32
BF16 = mybir.dt.bfloat16
I32 = mybir.dt.int32
U32 = mybir.dt.uint32
U16 = mybir.dt.uint16
U8 = mybir.dt.uint8
FP8X4 = mybir.dt.float8_e4m3fn_x4
ADD, MULT = mybir.AluOpType.add, mybir.AluOpType.mult
RELU = mybir.ActivationFunctionType.Relu
SQUARE = mybir.ActivationFunctionType.Square
COPY = mybir.ActivationFunctionType.Copy

P = 128
PACK = 4
WIDTH = 512
CHUNK = 512
PAIR = 2 * C
HALF = S // 2
BLOCKS = N // P
PAIRS = E // 2
QUADS = WIDTH // 4
REGION = 2 * PACK * WIDTH * 4
REGIONS = 5
EARLY_SPLIT = 40


def tile_moe_shr_mlp_relu2_kernel(tc, xT, w1, w2, gate, offs, out):
    nc = tc.nc
    with ExitStack() as ctx:
        held = ctx.enter_context(tc.tile_pool(name="held", bufs=1))
        rawp = ctx.enter_context(tc.tile_pool(name="rawp", bufs=1))
        late = ctx.enter_context(tc.tile_pool(name="late", bufs=1))
        spare = ctx.enter_context(tc.tile_pool(name="spare", bufs=1))
        xp = ctx.enter_context(tc.tile_pool(name="xp", bufs=1))
        two = ctx.enter_context(tc.tile_pool(name="two", bufs=2))
        three = ctx.enter_context(tc.tile_pool(name="three", bufs=3))
        ps_a = ctx.enter_context(tc.psum_pool(name="ps_a", bufs=6))
        ps_y = ctx.enter_context(tc.psum_pool(name="ps_y", bufs=2))

        offsets = held.tile([P, S // 16], U16, name="offsets")
        z = [held.tile([P, T], F32, name=f"z{b}") for b in range(BLOCKS)]
        nc.vector.memset(z[0][:], 0.0)
        nc.vector.memset(z[1][:], 0.0)
        nc.scalar.copy(out=z[2][:], in_=z[0][:])
        nc.gpsimd.memset(z[3][:], 0.0)

        gate_sb = held.tile([P, S], F32, name="gate_sb")
        planes = held.tile([P, 2 * T], U32, name="planes")

        def mx_tiles(pool, name, width):
            return (
                pool.tile([P, width], U32, name=name + "_codes", align_bytes=64),
                pool.tile([P, width], U8, name=name + "_scales", align_bytes=64),
            )

        slots = mx_tiles(held, "slot", S)
        tokens = mx_tiles(held, "token", T)
        ws1 = mx_tiles(held, "ws1", WIDTH)
        ws2 = mx_tiles(held, "ws2", WIDTH)

        def load(name, source, offset):
            raw = rawp.tile([P, PACK, source.shape[1]], F32, name=name, offset=offset)
            nc.sync.dma_start(out=raw[:], in_=source.rearrange("(p j) c -> p j c", j=PACK))
            return raw

        raws = {}
        order = [("w1", 0), ("w1", 1), ("w2", 0), ("w1", 2), ("w2", 1), ("w1", 3), ("w2", 2), ("w2", 3), ("w2", PAIRS)]

        def load_next():
            if len(raws) < len(order):
                kind, q = order[len(raws)]
                region = (len(raws) + 2) % REGIONS
                if q == PAIRS:
                    raws[kind, q] = load("shared_w2", w2[E], region * REGION)
                elif (kind, q) == ("w2", 0):
                    raws[kind, q] = load("w2_1", w2[1], region * REGION + REGION // 2)
                else:
                    raw = rawp.tile([P, 2, PACK, WIDTH], F32, name=f"raw{region}", offset=region * REGION)
                    source = (w1 if kind == "w1" else w2)[2 * q : 2 * q + 2].rearrange("e (p j) c -> p e j c", j=PACK)
                    if (kind, q) == ("w1", 0):
                        for u in range(2):
                            nc.sync.dma_start(out=raw[:, u], in_=source[:, u])
                    else:
                        nc.sync.dma_start(out=raw[:], in_=source)
                    raws[kind, q] = raw
                if (kind, q) == ("w2", 0):
                    nc.sync.dma_start(out=gate_sb[:], in_=gate[0:P, :])

        def copy_shared(dst, src, on_vector):
            if on_vector > 0:
                nc.vector.tensor_copy(out=dst[:, :on_vector], in_=src[:, :on_vector])
            if on_vector < src.shape[1]:
                nc.scalar.copy(out=dst[:, on_vector:], in_=src[:, on_vector:])

        def by_quads(raw):
            return raw.rearrange("p (g j) (m i) -> p m g i j", j=2, i=4)

        def plain(grouped):
            return grouped.rearrange("p (m i g j) -> p m g i j", i=4, g=2, j=2)

        def permuted(grouped):
            return grouped.rearrange("p (t m g j) -> p m g t j", t=PACK, g=2, j=2)

        def quantize(dst, cols, grouped):
            nc.vector.quantize_mx(out=dst[0][:, cols].bitcast(FP8X4), scales=dst[1][:, cols], in_=grouped)

        def mx(dst, w, wcols, x, xcols):
            nc.tensor.matmul_mx(
                out=dst,
                lhsT=w[0][:, wcols].bitcast(FP8X4),
                lhsT_scale=w[1][:, wcols],
                rhs=x[0][:, xcols].bitcast(FP8X4),
                rhs_scale=x[1][:, xcols],
                start=True,
                stop=True,
            )

        def first_layer(w, w0, x, x0, relu_out):
            bank = ps_a.tile([P, PACK, C], F32, name="bank_a")
            for t in range(PACK):
                mx(bank[:, t, :], w, slice(w0 + t * P, w0 + (t + 1) * P), x, slice(x0, x0 + C))
            nc.scalar.activation(relu_out.rearrange("p (c t) -> p c t", t=PACK), bank[:].rearrange("p t c -> p c t"), RELU)

        xb = {}

        def split_planes(c, t0, t1):
            nc.vector.tensor_copy(
                out=planes[:].bitcast(I32).rearrange("p (u t) -> p u t", u=2)[:, :, c * CHUNK + t0 : c * CHUNK + t1],
                in_=xb[c][:].bitcast(I32).rearrange("p (t u) -> p u t", u=2)[:, :, t0:t1],
            )

        def quantize_tokens(c, t0, t1):
            quantize(tokens, slice(c * CHUNK + t0, c * CHUNK + t1), xb[c][:, PACK * t0 : PACK * t1])

        hsb = {}

        def shared_first(c, parts=(0, 1), room=None):
            if 0 in parts:
                hsb[c] = three.tile([P, PACK * CHUNK], BF16, name="hsb", align_bytes=64)
            for a in parts:
                half = slice(a * PACK * PAIR, (a + 1) * PACK * PAIR)
                r = two.tile([P, PACK * PAIR], F32, name="r")[:] if room is None else room[:, half]
                for u in range(2):
                    first_layer(ws1, 0, tokens, c * CHUNK + a * PAIR + u * C, r[:, u * PACK * C : (u + 1) * PACK * C])
                nc.scalar.activation(hsb[c][:, half], r, SQUARE)

        hidden_s = {}

        def shared_hidden(c):
            at = {0: 1, 1: 3, 2: 4}[c] * REGION
            hidden_s[c] = (
                rawp.tile([P, CHUNK], U32, name=f"hs{c}_codes", align_bytes=64, offset=at),
                rawp.tile([P, CHUNK], U8, name=f"hs{c}_scales", align_bytes=64, offset=at + 4 * CHUNK),
            )
            quantize(hidden_s[c], slice(0, CHUNK), hsb[c][:])

        grouped = {}
        codes = {}
        hb = {}
        hq = {}
        yg = {}
        ONE = PACK * WIDTH

        def rounded(slot):
            return xp.tile([P, ONE], BF16, name=f"xb{slot}", align_bytes=64)

        def cast_w1(q, on_vector):
            if q == 1:
                grouped["w1", q] = late.tile([P, 2 * ONE], BF16, name="wb_second", align_bytes=64, offset=0)
            else:
                grouped["w1", q] = two.tile([P, 2 * ONE], BF16, name="wb", align_bytes=64)
            for u in range(2):
                copy_shared(permuted(grouped["w1", q][:, u * ONE : (u + 1) * ONE]), by_quads(raws["w1", q][:, u]), on_vector[u])
            load_next()

        def cast_w2(q):
            if q == 0:
                nc.vector.tensor_copy(out=plain(second[:]), in_=by_quads(raws["w2", q][:]))
                load_next()
                return
            if q == 2:
                grouped["w2", q] = late.tile([P, 2 * ONE], BF16, name="wb_late", align_bytes=64, offset=0)
            else:
                grouped["w2", q] = two.tile([P, 2 * ONE], BF16, name="wb", align_bytes=64)
            for a in range(2):
                nc.vector.tensor_copy(
                    out=grouped["w2", q][:, a * ONE : (a + 1) * ONE].rearrange("p (e m i j) -> p e m j i", e=2, i=4, j=PACK),
                    in_=raws["w2", q][:, :, :, a * PAIR : (a + 1) * PAIR].rearrange("p e j (m i) -> p e m j i", i=4),
                )
            load_next()

        def quantize_w(kind, q):
            if (kind, q) != ("w2", 0):
                codes[kind, q] = mx_tiles(two, kind, 2 * WIDTH)
            else:
                codes[kind, q] = (
                    late.tile([P, 2 * WIDTH], U32, name="first_codes", align_bytes=64, offset=0),
                    late.tile([P, 2 * WIDTH], U8, name="first_scales", align_bytes=64, offset=8 * WIDTH),
                )
                quantize(codes[kind, q], slice(0, WIDTH), early[:])
                routed_hidden(q)
                for a in range(2):
                    quantize(codes[kind, q], slice(WIDTH + a * PAIR, WIDTH + (a + 1) * PAIR), second[:, a * ONE // 2 : (a + 1) * ONE // 2])
                return
            for a in range(2):
                quantize(codes[kind, q], slice(a * WIDTH, (a + 1) * WIDTH), grouped[kind, q][:, a * ONE : (a + 1) * ONE])

        def routed_first(q):
            r = two.tile([P, PACK * PAIR], F32, name="r")
            for u in range(2):
                first_layer(codes["w1", q], u * WIDTH, slots, q * PAIR + u * C, r[:, u * PACK * C : (u + 1) * PACK * C])
            hb[q] = two.tile([P, PACK * PAIR], BF16, name="hb", align_bytes=64)
            nc.scalar.activation(hb[q][:], r[:], SQUARE)

        def routed_hidden(q):
            hq[q] = mx_tiles(held, "h", PAIR)
            quantize(hq[q], slice(0, PAIR), hb[q][:])

        def routed_second(q):
            yg[q] = two.tile([P, BLOCKS, PAIR], F32, name="yg")
            for a in range(2):
                bank = ps_y.tile([P, 2, PAIR], F32, name="bank_y")
                for i in range(2):
                    for u in range(2):
                        w0 = a * WIDTH + u * PAIR + i * P if q else u * WIDTH + a * PAIR + i * P
                        mx(bank[:, i, u * C : (u + 1) * C], codes["w2", q], slice(w0, w0 + P), hq[q], slice(u * C, (u + 1) * C))
                nc.vector.tensor_tensor(
                    out=yg[q][:, 2 * a : 2 * a + 2, :],
                    in0=bank[:],
                    in1=gate_sb[:, q * PAIR : (q + 1) * PAIR].unsqueeze(1).to_broadcast([P, 2, PAIR]),
                    op=MULT,
                )

        def scatter(q, b):
            o = offsets[:, q * (PAIR // 16) : (q + 1) * (PAIR // 16)]
            nc.scalar.activation(z[b][:].indirect(o), yg[q][:, b, :], COPY)

        quarter = REGION // 4
        ws1_raw = load("ws1", w1[E], 0)
        x_first = [load(f"x0_{h}", xT[:, h * PAIR : (h + 1) * PAIR], (2 + h) * quarter) for h in range(2)]
        x_raw = {1: load("x1", xT[:, CHUNK : 2 * CHUNK], REGION)}
        nc.sync.dma_start(offsets[:], offs)
        x_raw[2] = load("x2", xT[:, 2 * CHUNK :], REGION + 2 * quarter)
        early_raw = load("w2_0", w2[0], 4 * REGION)
        for n in range(REGIONS):
            load_next()

        wsb = rounded(0)
        copy_shared(permuted(wsb[:]), by_quads(ws1_raw[:]), 2 * EARLY_SPLIT)
        quantize(ws1, slice(0, WIDTH), wsb[:])
        xb[0] = rounded(1)
        copy_shared(plain(xb[0][:])[:, : QUADS // 2], by_quads(x_first[0][:]), EARLY_SPLIT)
        quantize_tokens(0, 0, PAIR)
        copy_shared(plain(xb[0][:])[:, QUADS // 2 :], by_quads(x_first[1][:]), EARLY_SPLIT)
        quantize_tokens(0, PAIR, CHUNK)
        shared_first(0)
        split_planes(0, 0, CHUNK)
        for c in (1, 2):
            xb[c] = rounded((c + 1) % 3)
            for h in range(2):
                quads = slice(h * QUADS // 2, (h + 1) * QUADS // 2)
                nc.vector.tensor_copy(out=plain(xb[c][:])[:, quads], in_=by_quads(x_raw[c][:])[:, quads])
            for h in range(2):
                split_planes(c, h * PAIR, (h + 1) * PAIR)
            quantize_tokens(c, 0, CHUNK)
        shared_first(1)
        early = rounded(0)
        nc.gpsimd.tensor_scalar(
            out=early[:].rearrange("p (c j) -> p c j", j=PACK),
            in0=early_raw[:].rearrange("p j c -> p c j"),
            scalar1=1.0,
            scalar2=0.0,
            op0=MULT,
            op1=ADD,
        )
        second = rounded(1)
        picked = late.tile([P, 2 * S], U32, name="picked", align_bytes=64, offset=0)
        halves = [slice(h * HALF, (h + 1) * HALF) for h in range(2)]
        nc.vector.tensor_copy(picked[:, :S], planes[:, :T].indirect(offsets[:]))
        for half in halves:
            o = offsets[:, half.start // 16 : half.stop // 16]
            nc.vector.tensor_copy(picked[:, S + half.start : S + half.stop], planes[:, T:].indirect(o))
        woven = spare.tile([P, PACK * S], BF16, name="woven", align_bytes=64, offset=0)
        for half in halves:
            nc.vector.tensor_copy(
                out=woven[:].bitcast(I32).rearrange("p (s u) -> p s u", u=2)[:, half],
                in_=picked[:].bitcast(I32).rearrange("p (u s) -> p s u", u=2)[:, half],
            )
        for half in halves:
            quantize(slots, half, woven[:, PACK * half.start : PACK * half.stop])
        cast_w1(0, (0, QUADS // 2))
        quantize_w("w1", 0)
        shared_first(2, (0, 1), raws["w1", 0][:, 0].rearrange("p j c -> p (j c)"))
        routed_first(0)

        for q in range(PAIRS):
            if q + 1 < PAIRS:
                cast_w1(q + 1, (QUADS, QUADS))
                quantize_w("w1", q + 1)
                routed_first(q + 1)
            if q > 0:
                routed_hidden(q)
            cast_w2(q)
            quantize_w("w2", q)
            if q > 0:
                shared_hidden(q - 1)
            routed_second(q)
            if q + 1 < PAIRS:
                for b in range(BLOCKS):
                    scatter(q, b)

        wsb = rounded(1)
        for h in range(2):
            quads = slice(h * QUADS // 2, (h + 1) * QUADS // 2)
            nc.vector.tensor_copy(out=plain(wsb[:])[:, quads], in_=by_quads(raws["w2", PAIRS][:])[:, quads])
        for h in range(2):
            quantize(ws2, slice(h * PAIR, (h + 1) * PAIR), wsb[:, h * ONE // 2 : (h + 1) * ONE // 2])

        for b in range(BLOCKS):
            scatter(PAIRS - 1, b)
            for c in range(T // CHUNK):
                bank = ps_a.tile([P, CHUNK], F32, name="bank_a")
                mx(bank[:], ws2, slice(b * P, (b + 1) * P), hidden_s[c], slice(0, CHUNK))
                cols = slice(c * CHUNK, (c + 1) * CHUNK)
                nc.vector.tensor_tensor(out=z[b][:, cols], in0=bank[:], in1=z[b][:, cols], op=ADD)
                nc.sync.dma_start(out=out[b * P : (b + 1) * P, cols], in_=z[b][:, cols])
